import numpy as np, ml_dtypes
CORES = [10,34,74,98]
N = 4
BF = ml_dtypes.bfloat16
def gentries(a):
    return np.ascontiguousarray(a.reshape(8, 16, -1).transpose(0, 2, 1)).reshape(8, -1)
def gtable(e):
    e = np.asarray(e); return np.ascontiguousarray(e.reshape(8, -1, 16).transpose(0, 2, 1)).reshape(128, -1).astype(np.int32)
W, L, M, RO = 4096, 256, 16, 6
def base(rng):
    x = rng.integers(0, 256, (N, 8, W, 16)); o = rng.permutation(W); h = W >> 3
    x[:, :, o[:h]] = x[:, :, o[h:2 * h]]
    ring = rng.integers(0, W, (N, 8, 16, L)); o = rng.permutation(L)
    ring[..., o[:4]] = ring[..., o[4:8]]
    return x, ring, rng.integers(0, 32, (N, 8, 16)), rng.integers(0, W >> 1, (N, 8, M))
def pack(x, ring, wt, kap):
    return {"x": np.ascontiguousarray(x.transpose(0, 1, 3, 2)).reshape(N, 128, W).astype(np.float32).astype(BF), "ring": np.ascontiguousarray(ring.reshape(N, 128, L)).astype(np.int32),
            "wt": np.ascontiguousarray(wt.reshape(N, 128, 1)).astype(np.int32), "kap": np.stack([gtable(a) for a in kap])}
def setup_inputs(rng):
    return pack(*base(rng))
def setup_inputs_spread(rng):
    x = np.minimum((np.exp2(8 * rng.random((N, 8, W, 1))) * rng.random((N, 8, W, 16)) * 1.25).astype(np.int64), 255) * (rng.random((N, 8, W, 1)) > 0.0625)
    low = np.minimum((W * rng.random((N, 8, 16, L)) ** 4).astype(np.int64), W - 1)
    ring = np.where(rng.random((N, 8, 1, L)) < 0.5, low, W - 1 - low)
    wt = np.minimum(np.exp2(5.2 * rng.random((N, 8, 16))).astype(np.int64), 31) * (rng.random((N, 8, 16)) > 0.125)
    kap = np.minimum(np.exp2(np.log2(W) * rng.random((N, 8, M))).astype(np.int64) - 1, W // 2 - 1)
    return pack(x, ring, wt, kap)
def setup_inputs_ends(rng):
    x = 255 * rng.integers(0, 2, (N, 8, W, 16)); q = rng.random((N, 8, W)); x[q < 0.25] = 0; x[q >= 0.75] = 255
    wt = 31 * rng.integers(0, 2, (N, 8, 16)); wt[:, 3] = 31; wt[:, 7] = 31; wt[:, 4] = 0
    kap = (W // 2 - 1) * rng.integers(0, 2, (N, 8, M))
    ring = (W - 1) * rng.integers(0, 2, (N, 8, 16, L)); mid = rng.random((N, 8, 16, L)) < 0.2
    for g in (0, 3, 7): mid[:, g] = False
    ring = np.where(mid, rng.integers(0, W, (N, 8, 16, L)), ring)
    c = (((W - 1) ** 2 >> 5) + kap * (W - 1) + (2 * np.arange(M) + 1) * (W - 1)) & (W - 1)
    for r in range(N):
        for g in (0, 3, 7):
            x[r, g, c[r, g]] = 0 if g == 0 else 255
            if g == 3: x[r, g, c[r, g, M - 1], int(rng.integers(0, 16))] = 254
            x[r, g, W - 1] = 0; x[r, g, 0] = 255
            for i in (2, 5, L - 1): ring[r, g, :2, i] = W - 1
            for i in (1, 8, L - 2): ring[r, g, :2, i] = 0
    return pack(x, ring, wt, kap)
def setup_inputs_corners(rng):
    x, ring, wt, kap = base(rng)
    for f_ in (0, 15): x[..., f_] = 32 * rng.integers(0, 8, (N, 8, W)) + rng.choice(np.array([0, 15, 16, 31, 1, 14, 17, 30]), (N, 8, W))
    for r in range(N):
        for g in range(8):
            k = (r + g) % 4; wt[r, g] = 31 if k == 2 else 0
            if k == 0: wt[r, g, 0] = 1
            if k == 3: wt[r, g, 15] = 1
            k = (r + g // 2) % 3; kap[r, g] = 0 if k == 0 else W // 2 - 1 if k == 1 else rng.choice(np.array([0, 1, W // 2 - 2, W // 2 - 1]), M)
    kind = rng.integers(0, 6, (N, 8, 1, L)); turn = (W - 1) * (np.arange(16) & 1)[None, None, :, None]
    ring = np.where(kind == 1, ring[:, :, :1], ring); ring = np.where(kind == 2, 0, ring); ring = np.where(kind == 3, W - 1, ring); ring = np.where(kind == 4, turn, ring)
    return pack(x, ring, wt, kap)
def setup_inputs_crowd(rng):
    x, ring, wt, kap = base(rng); wt[...] = 0; wt[..., 0] = 1; ring = np.minimum(ring, W - 2)
    i = int(rng.choice(np.array([0, L // 2, L - 1]))); sel = rng.integers(0, 4, L); o = 1 + rng.permutation(W - 2)
    for r in range(N):
        k = 3 if r == 3 else r % 3; up = 16 if k < 2 else 0
        x[r, ..., 0] = (x[r, ..., 0] & 3) + 2 if k == 3 else (x[r, ..., 0] & 239) + up
        for g in (0, 1): ring[r, g] = np.repeat(ring[r, g, :, :1].copy(), L, axis=1)
        ring[r, 1, :, i] = rng.integers(0, W - 1, 16)
        ring[r, 4] = ring[r, 4][:, sel]
        for g in (2, 3, 5, 7):
            v = int(rng.integers(1, W - 1)); x[r, g, v] = 0; x[r, g, v, 0] = 5 + up
            ring[r, g, 1] = v; ring[r, g, 5] = 0; kap[r, g] = 0
            if g in (3, 5): ring[r, g, 5, i] = int(rng.integers(1, W - 1))
        x[r, 6, :, 1] &= 127; x[r, 6, 0] = 0; x[r, 6, 0, 1] = 64; x[r, 6, o[0], 0] = 5 + up; x[r, 6, o[1], 0] = 6 + up
        ring[r, 6, 0] = o[0]; ring[r, 6, 1] = o[1]; ring[r, 6, 5] = 0; ring[r, 6, 6] = rng.permutation(o[2:])[:L]
        if k == 1: x[r, 6, W - 1, 0] = 5; ring[r, 6, 0, L - 1] = W - 1
        if k == 3: x[r, 4, W - 1, 0] = 16; ring[r, 4, 1, rng.permutation(L)[:int(rng.integers(1, 64))]] = W - 1
    return pack(x, ring, wt, kap)
def setup_inputs_ties(rng):
    x, ring, wt, kap = base(rng); pool = rng.integers(0, 256, (N, 8, 5, 16)); pool[:, :, 4] = (pool[:, :, 0] + pool[:, :, 1]) & 255
    pool[:, ::2, 3] = pool[:, ::2, 2] ^ 1
    x = np.take_along_axis(pool, rng.integers(0, 5, (N, 8, W, 1)), 2)
    for g in (1, 4, 7):
        ring[:, g] = rng.integers(0, 64, (N, 16, L))
        x[:, g, :64] = rng.integers(0, 4, (N, 64, 16)); x[:, g, 64:] = rng.integers(240, 256, (N, W - 64, 16))
    return pack(x, ring, wt, kap)
def check_inputs(d):
    bad = []
    for k, lo, hi in (("x", 0, 255), ("ring", 0, W - 1), ("wt", 0, 31), ("kap", 0, W // 2 - 1)):
        a = np.asarray(d[k]).astype(np.float32)
        if not (np.min(a) >= lo and np.max(a) <= hi): bad.append("range of " + k)
        elif np.any(a != np.floor(a)): bad.append("whole numbers of " + k)
    return bad
def pick(X, ix):
    return np.take_along_axis(X, ix[..., None], 2)
def reference(x, ring, wt, kap):
    X = np.ascontiguousarray(x.astype(np.float32).astype(np.int32).reshape(N, 8, 16, W).transpose(0, 1, 3, 2))
    R = ring.astype(np.int64).reshape(N, 8, 16, L); wts = wt.astype(np.int32).reshape(N, 8, 1, 16)
    kp = np.stack([gentries(a) for a in kap]).astype(np.int64)[:, :, None, :]; odd = 2 * np.arange(M) + 1
    A = np.zeros(N, np.int64)
    for t in range(RO):
        far = np.stack([R[(r + 1 + t % (N - 1)) % N] for r in range(N)])
        both = np.concatenate([R, far], axis=2)
        a = (np.add.reduce(pick(X, R[:, :, 0]) * wts, axis=3) & 31).astype(np.int64)
        b = (np.add.reduce(pick(X, R[:, :, 1]) * wts, axis=3) & 31).astype(np.int64)
        P = np.take_along_axis(both, a[:, :, None, :], 2)[:, :, 0]; Q = np.take_along_axis(both, b[:, :, None, :], 2)[:, :, 0]
        y = (pick(X, P) + pick(X, Q)) & 255
        c = (((P * Q) >> 5)[..., None] + kp * P[..., None] + odd * Q[..., None] + A[:, None, None, None]) & (W - 1)
        s = np.add.reduce(np.abs(pick(X, c.reshape(N, 8, L * M)).reshape(N, 8, L, M, 16) - y[:, :, :, None, :]), axis=4)
        m = np.argmin(s, axis=3)
        e = np.take_along_axis(c, m[..., None], 3)[..., 0]
        A = np.add.reduce(((a >= 16).astype(np.int64) + (b >= 16)).reshape(N, 8 * L), axis=1) & 63
        for r in range(N):
            for g in range(8):
                v, i = np.unique(e[r, g], return_index=True)
                X[r, g, v] = (X[r, g, v] + y[r, g, i]) >> 1
        R = np.concatenate([e[:, :, None, :], R[:, :, :15]], axis=2)
    return {"yx": np.ascontiguousarray(X.transpose(0, 1, 3, 2)).reshape(N, 128, W).astype(np.float32).astype(BF), "yr": R.reshape(N, 128, L).astype(np.float32)}

@@ -1,0 +1,413 @@
+from concourse.mybir import AluOpType, AxisListType, ActivationFunctionType
+
+OP = AluOpType
+AF = ActivationFunctionType
+STEPS = 6
+SO = 21
+S2 = 5
+FOREIGN = [(k, s) for k in range(3) for s in range(STEPS - 1) if any(t > s for t in (k, k + 3))]
+A_PIECES = [(208, 32)]
+PIECES = [(0, 32), (208, 32), (32, 32), (64, 32), (96, 32), (128, 32), (160, 32), (192, 16), (240, 16)]
+BANKS = ["pD0", "pD1", "pD2", "pD3", "pL", "pR"]
+SCORE_AT = {4: 0, 6: 1, 8: 2}
+
+F4, B2, F2, I4, U2 = "float32", "bfloat16", "float16", "int32", "uint16"
+SCRATCH = {}
+for _n, _w, _d in [
+        ("X", 4128, B2), ("RW", 53 * 256, F4), ("RW2", 37 * 256, F4), ("ri", 256, I4), ("r16", 256, F2), ("zz", 512, F2),
+        ("wti", 1, I4), ("kpi", 1, I4), ("kpb", 1, I4), ("U", 2048, F2), ("L", 2048, F2), ("WD", 2048, B2), ("E", 2048, B2),
+        ("one", 512, B2), ("I16", 128, F2), ("KD", 128, F2), ("OD", 128, F2), ("AD", 128, F2), ("B16", 128, F2),
+        ("IB", 128, B2), ("NI", 128, B2), ("PI", 128, B2), ("MI", 128, B2), ("ip", 1, I4), ("ipg", 1, I4), ("ipm", 1, I4),
+        ("inn", 128, I4), ("ig", 128, I4), ("iL", 128, I4), ("iU", 128, I4), ("i32", 32, I4), ("i16", 16, I4), ("i1", 16, I4),
+        ("iq", 256, I4), ("i24", 24, I4), ("in3", 384, I4), ("colU", 16, F4), ("colL", 16, F4), ("pc", 1, F4), ("pg", 1, F4),
+        ("pm", 1, F4), ("pm16", 1, F4), ("is0", 1, F4), ("is1", 1, F4), ("dmE", 1, F4), ("dmO", 1, F4), ("wf", 1, F4), ("wg", 1, F4),
+        ("wh", 1, F4), ("kf", 1, F4), ("kg", 1, F4), ("kh", 1, F4), ("odd", 1, F4), ("cc0", 1, F4), ("acc", 1, F4),
+        ("cntf", 1, F4), ("cnti", 1, I4), ("cnta", 1, I4), ("LANE", 32, F2), ("C4", 32, B2), ("MC", 256, F2), ("RS", 256, F4),
+        ("HOLD", 384, F4), ("MK", 384, F4), ("CL", 24, U2), ("OH", 16, B2), ("ELI", 32, U2), ("EL", 16 * STEPS, U2),
+        ("Ga", 512, B2), ("xi", 32, I4), ("xj", 32, I4), ("RL", 32, U2), ("flg", 32, B2), ("PQ", 512, F2), ("PL", 32, U2),
+        ("pr", 256, I4), ("sh", 256, I4), ("ci", 256, I4), ("cj", 256, I4), ("cl", 256, U2), ("c16", 256, F2), ("XPQ", 512, B2),
+        ("sg", 256, B2), ("YT", 256, B2), ("G", 4096, B2), ("mn", 256, F4), ("ki", 16, I4), ("kj", 16, I4), ("ML", 16, U2),
+        ("z", 256, F2), ("ewf", 16, F4), ("e16", 16 * STEPS, F2), ("ER", 384, F4), ("eq", 384, B2), ("lo", 384, F4),
+        ("tx", 16, F4), ("off", 16, U2), ("XE", 256, B2), ("nx", 256, I4),
+        ("LR0", 256, F2), ("LR1", 256, F2), ("LR2", 256, F2)] + [("LE%d%d" % ks, 16, F2) for ks in FOREIGN]:
+    SCRATCH[_n] = ("sbuf", [128, _w], _d)
+SCRATCH["MA"] = ("sbuf", [128, 256, 16], B2)
+for _n in ("pA", "pL", "pR", "pS", "pD0", "pD1", "pD2", "pD3"):
+    SCRATCH[_n] = ("psum", [128, 512], F4)
+SEMAPHORES = (["sv", "sa", "sp", "sq", "dr", "dx", "dw", "dk", "d2", "dy", "dz", "loc"] + ["ar%d" % k for k in range(3)]
+              + ["ae%d%d" % ks for ks in FOREIGN])
+
+
+def rank_program(g, core, T, topo):
+    rank = T.rank_of(core)
+    if rank is None:
+        return
+    n_ranks = len(T.cores)
+    eng = {"v": g.vector, "a": g.scalar, "p": g.tensor, "q": g, "s": g.sync}
+    sem = {"v": "sv", "a": "sa", "p": "sp", "q": "sq"}
+    count = {"v": 0, "a": 0, "p": 0, "q": 0}
+    know = {e: {} for e in eng}
+    lastw, readers, bank = {}, {}, {}
+
+    def need(e, token):
+        name, n, clock = token
+        if know[e].get(name, 0) >= n:
+            return
+        eng[e].wait_ge(T.sem[name], n)
+        for s_, n_ in list(clock.items()) + [(name, n)]:
+            if know[e].get(s_, 0) < n_:
+                know[e][s_] = n_
+
+    def before(e, R, W, banks):
+        own = sem.get(e)
+        deps = [lastw[r] for r in R if r in lastw]
+        deps += [lastw[w] for w in W if w in lastw and (e != "p" or lastw[w][0] != own)]
+        for w in W:
+            deps += [t for t in readers.get(w, []) if t[0] != own]
+        for b in banks:
+            deps += [t for x, t in bank.get(b, {}).items() if x != e]
+        for t in sorted(deps, key=lambda t: -t[1]):
+            need(e, t)
+
+    def after(e, token, R, W, banks):
+        for w in W:
+            lastw[w] = token
+            readers[w] = []
+        for r in R:
+            readers.setdefault(r, []).append(token)
+        for b in banks:
+            bank.setdefault(b, {})[e] = token
+
+    def op(e, calls, R=(), W=(), B=()):
+        before(e, R, W, B)
+        for c in (calls if isinstance(calls, list) else [calls]):
+            i = c()
+        count[e] += 1
+        i.then_inc(T.sem[sem[e]], 1)
+        after(e, (sem[e], count[e], dict(know[e])), R, W, B)
+
+    def dma(e, out, in_, s, R=(), W=()):
+        before(e, R, W, ())
+        eng[e].dma_start(out, in_).then_inc(T.sem[s], 16)
+        after(e, (s, 16, dict(know[e])), R, W, ())
+
+    V, A, P = g.vector, g.scalar, g.tensor
+
+    def ts(out, in0, s1, op0, R, W, s2=None, op1=None, B=()):
+        if op1 is None:
+            op("v", lambda: V.tensor_scalar(out, in0, s1, None, op0), R, W, B)
+        else:
+            op("v", lambda: V.tensor_scalar(out, in0, s1, s2, op0, op1), R, W, B)
+
+    def tt(out, in0, in1, o, R, W, B=()):
+        op("v", lambda: V.tensor_tensor(out, in0, in1, o), R, W, B)
+
+    def cp(out, in_, R, W, B=()):
+        op("v", lambda: V.tensor_copy(out, in_), R, W, B)
+
+    def act(out, in_, f, R, W, B=(), bias=0.0):
+        op("a", lambda: A.activation(out, in_, f, bias=bias), R, W, B)
+
+    def mm(out, lhsT, rhs, start, stop):
+        return lambda: P.matmul(out, lhsT, rhs, start, stop)
+
+    def blk(t, q):
+        return t[:, 128 * q:128 * q + 128]
+
+    loc = [0]
+
+    def send(k, dst_t, src, s, R):
+        dst = T.cores[(rank - 1 - k) % n_ranks]
+        rid, pid, _ = topo.addr(dst)
+        before("q", R, (), ())
+        g.remote_dma(dst_t, src, T.sem[s], T.sem.loc, pid, rid, topo.mask(core, dst))
+        loc[0] += len(topo.engines(core, dst))
+
+    def arrived(k, s, key):
+        src = T.cores[(rank + 1 + k) % n_ranks]
+        lastw[key] = (s, len(topo.engines(src, core)), {})
+
+    def iota(name, pattern, base, cm, cols=None):
+        out = T[name][:] if cols is None else T[name][:, cols[0]:cols[1]]
+        if name == "colU":
+            op("q", lambda: g.iota(out, pattern, base, cm, allow_small_or_imprecise_dtypes=True), W=[name])
+        else:
+            op("q", lambda: g.iota(out, pattern, base, cm), W=[name])
+
+    dma("s", T.ri[:], T.ring[:], "dr", W=["ri"])
+    dma("a", T.wti[:], T.wt[:], "dw", W=["wti"])
+    dma("a", T.kpi[:], T.kap[:], "dk", W=["kpi"])
+    dma("s", T.X[:, 0:4096], T.x[:], "dx", W=["X"])
+    iota("ip", [[0, 1]], 0, 1)
+    iota("colU", [[-1, 16]], 0, 1)
+    iota("iU", [[16, 8], [0, 16]], 0, 0)
+    iota("i16", [[16, 16]], 0, 0)
+    iota("iL", [[1, 8], [16, 16]], 0, 0)
+    iota("inn", [[1, 128]], 0, 0)
+    iota("i32", [[0, 2], [16, 16]], 0, 0)
+    iota("i1", [[1, 16]], 0, 0)
+    ts(T.ipg[:], T.ip[:], 4, OP.arith_shift_right, ["ip"], ["ipg"])
+    ts(T.ipm[:], T.ip[:], 15, OP.bitwise_and, ["ip"], ["ipm"])
+    cp(T.pc[:], T.ip[:], ["ip"], ["pc"])
+    cp(T.pg[:], T.ipg[:], ["ipg"], ["pg"])
+    cp(T.pm[:], T.ipm[:], ["ipm"], ["pm"])
+    ts(T.colL[:], T.i16[:], T.pg[:], OP.add, ["i16", "pg"], ["colL"])
+    ts(T.is0[:], T.pm[:], 0.0, OP.is_equal, ["pm"], ["is0"])
+    ts(T.is1[:], T.pm[:], 1.0, OP.is_equal, ["pm"], ["is1"])
+    for q in range(16):
+        if q == 9:
+            ts(T.r16[:], T.ri[:], -2048.0, OP.add, ["ri"], ["r16"])
+        ts(blk(T.U, q), T.iU[:], T.colU[:, q:q + 1], OP.is_equal, ["iU", "colU"], ["U%d" % q])
+    for k in range(3):
+        send(k, T["LR%d" % k][:], T.r16[:], "ar%d" % k, ["r16"])
+        arrived(k, "ar%d" % k, "LR%d" % k)
+    iota("iq", [[0, 16], [1, 16]], 0, 0)
+    op("v", lambda: V.memset(T.one[:], 1.0), W=["one"])
+    for j in range(4):
+        op("q", lambda: g.affine_select(T.E[:, 512 * j:512 * j + 512], T.one[:], [[-1, 32], [0, 16]], OP.is_equal, 0.0, -32 * j, 1), ["one"], ["E%d" % j])
+    iota("in3", [[0, 8], [1, 32]], 0, 0, (0, 256))
+    iota("in3", [[0, 8], [1, 16]], 16, 0, (256, 384))
+    iota("i24", [[2, 8], [0, 2]], 1, 0, (0, 16))
+    iota("i24", [[2, 8]], 0, 0, (16, 24))
+
+    D = [T.pD0, T.pD1, T.pD2, T.pD3]
+    dn = [0]
+
+    def spread(src, key, buf, bkey, slot, ages, pairs, copier="a"):
+        for j in pairs:
+            w = min(2, ages - 2 * j)
+            d = dn[0] % 4
+            dn[0] += 1
+            bk = "pD%d" % d
+            op("p", [mm(D[d][:, 256 * i:256 * i + 256], blk(T.U, 2 * j + i), src[:], True, True) for i in range(w)],
+               [key] + ["U%d" % (2 * j + i) for i in range(w)], [bk], [bk])
+            o = buf[:, (slot + 2 * j) * 256:(slot + 2 * j + w) * 256]
+            ws = [bkey + "s%d" % (slot + 2 * j + i) for i in range(w)]
+            if copier == "v":
+                ts(o, D[d][:, 0:256 * w], 2048.0, OP.add, [bk], ws, B=[bk])
+            else:
+                act(o, D[d][:, 0:256 * w], AF.Copy, [bk], ws, [bk], bias=2048.0)
+
+    spread(T.r16, "r16", T.RW, "RW", SO, 16, range(8))
+    dma("s", T.RW2[:, S2 * 256:(S2 + 14) * 256], T.RW[:, SO * 256:(SO + 14) * 256], "d2",
+        ["RWs%d" % (SO + i) for i in range(14)], ["RW2s%d" % (S2 + i) for i in range(14)])
+    for q in range(16):
+        ts(blk(T.L, q), T.iL[:], T.colL[:, q:q + 1], OP.is_equal, ["iL", "colL"], ["L"] if q == 15 else ["L_%d" % q])
+    ts(T.zz[:, 0:256], T.r16[:], T.is0[:], OP.mult, ["r16", "is0"], ["zz0"])
+    ts(T.zz[:, 256:512], T.r16[:], T.is1[:], OP.mult, ["r16", "is1"], ["zz1"])
+    op("p", [mm(T.pA[:, 64:96], blk(T.L, q), T.zz[:, q::16], q == 0, q == 15) for q in range(16)], ["zz0", "zz1", "L"], ["pA"], ["pA"])
+    cp(T.wf[:], T.wti[:], ["wti"], ["wf"])
+    ts(T.wh[:], T.wf[:], 256.0, OP.mult, ["wf"], ["wh"])
+    ts(T.wg[:], T.wf[:], 16.0, OP.is_ge, ["wf"], ["wg"], -8192.0, OP.mult)
+    ts(T.I16[:], T.inn[:], T.pc[:], OP.is_equal, ["inn", "pc"], ["I16"])
+    tt(T.wf[:], T.wh[:], T.wg[:], OP.add, ["wh", "wg"], ["wf"])
+    ts(T.LANE[:], T.i32[:], T.pm[:], OP.add, ["i32", "pm"], ["LANE"])
+    ts(T.ELI[:], T.pA[:, 64:96], 2048.0, OP.add, ["pA"], ["ELI"], B=["pA"])
+    ts(T.WD[:], T.L[:], T.wf[:], OP.mult, ["L", "wf"] + ["L_%d" % q for q in range(15)], ["WD"])
+
+    def constants(part):
+        if part == 0:
+            cp(T.kf[:], T.kpi[:], ["kpi"], ["kf"])
+            ts(T.kpb[:], T.kpi[:], 1, OP.bitwise_and, ["kpi"], ["kpb"])
+            ts(T.kg[:], T.kf[:], 1985.0, OP.is_ge, ["kf"], ["kg"], -4096.0, OP.mult)
+            ts(T.kh[:], T.kf[:], 64.0, OP.add, ["kf"], ["kh"])
+            ts(T.cc0[:], T.kpb[:], 2048.0, OP.mult, ["kpb"], ["cc0"], -2048.0, OP.add)
+            ts(T.odd[:], T.pm[:], 2.0, OP.mult, ["pm"], ["odd"], 65.0, OP.add)
+            tt(T.kf[:], T.kh[:], T.kg[:], OP.add, ["kh", "kg"], ["kf"])
+            ts(T.AD[:], T.I16[:], T.cc0[:], OP.mult, ["I16", "cc0"], ["AD"])
+            ts(T.OD[:], T.I16[:], T.odd[:], OP.mult, ["I16", "odd"], ["OD"])
+            ts(T.KD[:], T.I16[:], T.kf[:], OP.mult, ["I16", "kf"], ["KD"])
+            cp(T.IB[:], T.I16[:], ["I16"], ["IB"])
+            ts(T.NI[:], T.I16[:], -1.0, OP.mult, ["I16"], ["NI"])
+            ts(T.PI[:], T.I16[:], 128.0, OP.mult, ["I16"], ["PI"])
+        elif part == 1:
+            ts(T.MC[:], T.iq[:], 0.03125, OP.mult, ["iq"], ["MC"])
+            ts(T.MI[:], T.I16[:], -128.0, OP.mult, ["I16"], ["MI"])
+        else:
+            ts(T.ig[:], T.inn[:], 4, OP.arith_shift_right, ["inn"], ["ig"])
+            ts(T.pm16[:], T.pm[:], 16.0, OP.add, ["pm"], ["pm16"])
+            ts(T.dmE[:], T.pm[:], 4096.0, OP.add, ["pm"], ["dmE"])
+            ts(T.dmO[:], T.pm[:], 4112.0, OP.add, ["pm"], ["dmO"])
+            ts(T.RS[:], T.iq[:], 0.0, OP.is_equal, ["iq"], ["RS"], 1.0e9, OP.mult)
+            ts(T.B16[:], T.ig[:], T.pg[:], OP.is_equal, ["ig", "pg"], ["B16"])
+            ts(T.HOLD[:, 0:256], T.in3[:, 0:256], 0.0, OP.is_gt, ["in3"], ["HOLDO"])
+            ts(T.HOLD[:, 256:384], T.in3[:, 256:384], 16.0, OP.is_gt, ["in3"], ["HOLDE"])
+            ts(T.MK[:], T.in3[:], T.pm16[:], OP.is_ge, ["in3", "pm16"], ["MK"], 8192.0, OP.mult)
+            ts(T.HOLD[:, 31:256:32], T.in3[:, 31:256:32], 0.0, OP.mult, ["in3", "dmO"], ["HOLDO"], T.dmO[:], OP.add)
+            ts(T.HOLD[:, 271:384:16], T.in3[:, 271:384:16], 0.0, OP.mult, ["in3", "dmE"], ["HOLDE"], T.dmE[:], OP.add)
+            ts(T.MK[:], T.MK[:], 2048.0, OP.add, ["MK"], ["MK"])
+            cp(T.CL[:], T.i24[:], ["i24"], ["CL"])
+            ts(T.OH[:], T.i1[:], T.pm[:], OP.is_equal, ["i1", "pm"], ["OH"])
+
+    def el(s):
+        if s >= 0:
+            return T.EL[:, 16 * s:16 * s + 16], "EL%d" % s
+        return (T.ELI[:, 0:16] if s == -1 else T.ELI[:, 16:32]), "ELI"
+
+    Xw = T.X[:, 0:4096]
+    pushed = set()
+
+    def push_foreign(k, s):
+        pushed.add((k, s))
+        key = "LE%d%d" % (k, s)
+        buf, bkey, slot = [(T.RW, "RW", SO + 15 - s), (T.RW, "RW", SO - 17 - s), (T.RW2, "RW2", S2 + 15 - s)][k]
+        arrived(k, "ae%d%d" % (k, s), key)
+        op("p", [mm(T.pR[:, q:256:16], blk(T.U, q), T[key][:], True, True) for q in range(16)],
+           [key] + ["U%d" % q for q in range(16)], ["pR"], ["pR"])
+        return lambda: act(buf[:, slot * 256:slot * 256 + 256], T.pR[:, 0:256], AF.Copy, ["pR"], [bkey + "s%d" % slot], ["pR"], bias=2048.0)
+
+    def pkey(name, l0, n):
+        return ["%s%d" % (name, c) for c in range(l0 // 16, (l0 + n) // 16)]
+
+    for t in range(STEPS):
+        k = t % 3
+        last = t == STEPS - 1
+        la, lka = el(t - 1)
+        lb, lkb = el(t - 2)
+        put = None
+        if t > 0 and (k, t - 1) not in pushed:
+            put = push_foreign(k, t - 1)
+        cp(T.Ga[:, 0:256], Xw.indirect(la), ["X", lka], ["Ga0"])
+        if t == 0:
+            cp(T.Ga[:, 256:512], Xw.indirect(lb), ["X", lkb], ["Ga1"])
+            spread(T.LR0, "LR0", T.RW, "RW", SO + 16, 16, range(4))
+            constants(0)
+        else:
+            act(T.Ga[:, 256:512], Xw.indirect(lb), AF.Copy, ["X", lkb], ["Ga1"])
+        if put:
+            put()
+        ms = [mm(T.pA[:, 0:32], T.I16[:], T.LANE[:], True, False)]
+        if k == 1:
+            ms.append(mm(T.pA[:, 0:32], T.I16[:], T.C4[:], False, False))
+        op("p", ms, ["I16", "LANE", "C4"], ["pA"], ["pA"])
+        op("p", [mm(T.pA[:, 0:32], blk(T.WD, q), T.Ga[:, q::16], False, q == 15) for q in range(16)], ["WD", "Ga0", "Ga1"], ["pA"], ["pA"])
+        cp(T.xi[:], T.pA[:, 0:32], ["pA"], ["xi"], ["pA"])
+        ts(T.xj[:], T.xi[:], 8191, OP.bitwise_and, ["xi"], ["xj"])
+        cp(T.RL[:], T.xj[:], ["xj"], ["RL"])
+        if t == 0:
+            spread(T.LR0, "LR0", T.RW, "RW", SO + 16, 16, (4, 5))
+            spread(T.LR0, "LR0", T.RW, "RW", SO + 16, 16, (6, 7), "v")
+            op("v", lambda: V.memset(T.C4[:], 4096.0), W=["C4"])
+        buf, rk, w0 = [(T.RW, "RW", SO - t), (T.RW, "RW", SO - 16 - t), (T.RW2, "RW2", S2 - t)][k]
+        ts(T.PQ[:], buf[:, w0 * 256:(w0 + 32) * 256].indirect(T.RL[:]), -2048.0, OP.add, ["RL"] + [rk + "s%d" % i for i in range(w0, w0 + 32)], ["PQ"])
+        op("p", [mm(T.pA[:, 64:96], blk(T.L, q), T.PQ[:, q::16], q == 0, q == 15) for q in range(16)], ["PQ", "L"], ["pA"], ["pA"])
+        op("p", [mm(T.pL[:, 0:256], T.KD[:], T.PQ[:, 0:256], True, False), mm(T.pL[:, 0:256], T.OD[:], T.PQ[:, 256:512], False, False),
+                 mm(T.pL[:, 0:256], T.AD[:], T.one[:, 0:256], False, True)], ["PQ", "KD", "OD", "AD", "one"], ["pL"], ["pL"])
+        tt(T.pr[:], T.PQ[:, 0:256], T.PQ[:, 256:512], OP.mult, ["PQ"], ["pr"])
+        if not last:
+            ts(T.flg[:], T.xj[:], 4096.0, OP.is_lt if k == 1 else OP.is_ge, ["xj"], ["flg"])
+        ts(T.PL[:], T.pA[:, 64:96], 0.0625, OP.mult, ["pA"], ["PL"], 2048.0, OP.add, B=["pA"])
+        ts(T.sh[:], T.pr[:], 5, OP.arith_shift_right, ["pr"], ["sh"])
+        tt(T.ci[:], T.sh[:], T.pL[:, 0:256], OP.add, ["sh", "pL"], ["ci"], ["pL"])
+        ts(T.cj[:], T.ci[:], 4095, OP.bitwise_and, ["ci"], ["cj"])
+        cp(T.cl[:], T.cj[:], ["cj"], ["cl"])
+        if t == 0:
+            constants(1)
+        act(T.XPQ[:], Xw.indirect(T.PL[:]), AF.Copy, ["X", "PL"], ["XPQ"])
+        op("p", [mm(T.pS[:, 0:256], T.IB[:], T.XPQ[:, 0:256], True, False), mm(T.pS[:, 0:256], T.IB[:], T.XPQ[:, 256:512], False, True)],
+           ["XPQ", "IB"], ["pS"], ["pS"])
+        act(T.sg[:], T.pS[:, 0:256], AF.Sign, ["pS"], ["sg"], ["pS"], bias=-255.5)
+        ms = []
+        for h in range(2):
+            o = T.pS[:, 256 + 128 * h:384 + 128 * h]
+            ms += [mm(o, T.XPQ[:, 128 * h:128 * h + 128], T.NI[:], True, False),
+                   mm(o, T.XPQ[:, 256 + 128 * h:384 + 128 * h], T.NI[:], False, False),
+                   mm(o, T.sg[:, 128 * h:128 * h + 128], T.PI[:], False, True)]
+        op("p", ms, ["XPQ", "sg", "NI", "PI"], ["pS"], ["pS"])
+        act(T.YT[:], T.pS[:, 256:512], AF.Copy, ["pS"], ["YT"], ["pS"], bias=128.0)
+        for l0, n in PIECES:
+            o, i = T.G[:, 16 * l0:16 * (l0 + n)], Xw.indirect(T.cl[:, l0:l0 + n])
+            if (l0, n) in A_PIECES:
+                act(o, i, AF.Copy, ["X", "cl"], pkey("G", l0, n))
+            else:
+                cp(o, i, ["X", "cl"], pkey("G", l0, n))
+
+        def yexp(s):
+            l0, n = PIECES[s]
+            bk, h = BANKS[s % len(BANKS)], l0 % 128
+            op("p", mm(T[bk][:, 0:16 * n], blk(T.YT, l0 // 128), T.E[:, 16 * h:16 * (h + n)], True, False),
+               ["YT"] + ["E%d" % j for j in range(h // 32, (h + n + 31) // 32)], [bk], [bk])
+
+        def score(Q):
+            op("p", [mm(T.pS[:, 64 * Q:64 * Q + 64], blk(T.L, q), T.MA[:, 64 * Q + q:64 * Q + 64:16, :], False, Q == 3 and q == 15)
+                     for q in range(16)], ["L"] + pkey("MA", 64 * Q, 64), ["pS"], ["pS"])
+        yexp(0)
+        yexp(1)
+        for s, (l0, n) in enumerate(PIECES):
+            bk = BANKS[s % len(BANKS)]
+            d = T[bk][:, 0:16 * n]
+            op("p", mm(d, T.IB[:], T.G[:, 16 * l0:16 * (l0 + n)], False, True), ["IB"] + pkey("G", l0, n), [bk], [bk])
+            act(T.MA[:, l0:l0 + n, :], d, AF.Abs, [bk], pkey("MA", l0, n), [bk])
+            if s == 1:
+                for x in range(2, len(BANKS)):
+                    yexp(x)
+                op("p", mm(T.pS[:, 0:256], T.I16[:], T.MC[:], True, False), ["I16", "MC"], ["pS"], ["pS"])
+                if not last:
+                    op("p", mm(T.pA[:, 160:192], T.one[:, 0:128], T.flg[:], True, True), ["one", "flg"], ["pA"], ["pA"])
+            if s >= 2 and s - 2 + len(BANKS) < len(PIECES):
+                yexp(s - 2 + len(BANKS))
+            if s in SCORE_AT:
+                score(SCORE_AT[s])
+        score(3)
+        op("p", [mm(T.pL[:, 0:256], T.IB[:], T.XPQ[:, 0:256], True, False), mm(T.pL[:, 0:256], T.IB[:], T.XPQ[:, 256:512], False, False),
+                 mm(T.pL[:, 0:256], T.MI[:], T.sg[:], False, False)], ["IB", "MI", "XPQ", "sg"], ["pL"], ["pL"])
+        if t == 0:
+            constants(2)
+        ts(T.c16[:], T.cj[:], -2048.0, OP.add, ["cj"], ["c16"])
+        if not last:
+            op("v", lambda: V.tensor_reduce(T.cntf[:], T.pA[:, 160:192], AxisListType.X, OP.add), ["pA"], ["cntf"], ["pA"])
+            cp(T.cnti[:], T.cntf[:], ["cntf"], ["cnti"])
+            ts(T.cnta[:], T.cnti[:], 63, OP.bitwise_and, ["cnti"], ["cnta"])
+            tt(T.acc[:], T.cnta[:], T.cc0[:], OP.add, ["cnta", "cc0"], ["acc"])
+            ts(T.AD[:], T.I16[:], T.acc[:], OP.mult, ["I16", "acc"], ["AD"])
+        if t == 0:
+            spread(T.LR1, "LR1", T.RW, "RW", SO - 16, 15, range(4))
+        if t == 1:
+            spread(T.LR2, "LR2", T.RW2, "RW2", S2 + 16, 14, range(4))
+        op("v", lambda: V.tensor_tensor_scan(T.mn[:], T.RS[:], T.pS[:, 0:256], 0.0, OP.max, OP.min), ["RS", "pS"], ["mn"], ["pS"])
+        ts(T.ki[:], T.mn[:, 15::16], 32.0, OP.mult, ["mn"], ["ki"])
+        ts(T.kj[:], T.ki[:], 15, OP.bitwise_and, ["ki"], ["kj"])
+        cp(T.ML[:], T.kj[:], ["kj"], ["ML"])
+        tt(T.z[:], T.OH[:].indirect(T.ML[:]), T.c16[:], OP.mult, ["OH", "ML", "c16"], ["z"])
+        op("p", [mm(T.pA[:, 128:144], blk(T.L, q), T.z[:, q::16], q == 0, q == 15) for q in range(16)], ["L", "z"], ["pA"], ["pA"])
+        op("p", [mm(T.pR[:, 256 + 16 * b:272 + 16 * b], T.B16[:], T.z[:, 32 * b:32 * b + 16], True, True) for b in range(8)]
+           + [mm(T.pR[:, 0:256], T.B16[:], T.z[:], True, True)], ["B16", "z"], ["pR"], ["pR"])
+        en, ek = el(t)
+        ts(en, T.pA[:, 128:144], 2048.0, OP.add, ["pA"], [ek], B=["pA"])
+        ts(T.ewf[:], T.pA[:, 128:144], 2048.0, OP.add, ["pA"], ["ewf"], B=["pA"])
+        act(T.XE[:], Xw.indirect(en), AF.Copy, ["X", ek], ["XE"])
+        op("p", mm(T.pL[:, 0:256], T.IB[:], T.XE[:], False, True), ["IB", "XE"], ["pL"], ["pL"])
+        if not last:
+            cp(T.e16[:, 16 * t:16 * t + 16], T.pA[:, 128:144], ["pA"], ["e16%d" % t], ["pA"])
+            for kk in sorted(range(3), key=lambda x: (x - t - 1) % 3):
+                if (kk, t) in FOREIGN:
+                    send(kk, T["LE%d%d" % (kk, t)][:], T.e16[:, 16 * t:16 * t + 16], "ae%d%d" % (kk, t), ["e16%d" % t])
+        tt(T.ER[:], T.pR[:, 0:384], T.MK[:], OP.add, ["pR", "MK"], ["ER"], ["pR"])
+        tt(T.eq[:], T.ewf[:].indirect(T.CL[:]), T.ER[:], OP.is_equal, ["ewf", "CL", "ER"], ["eq"])
+        ts(T.nx[:], T.pL[:, 0:256], 0.5, OP.mult, ["pL"], ["nx"], -64.25, OP.add, B=["pL"])
+        op("v", lambda: V.tensor_tensor_scan(T.lo[:], T.HOLD[:], T.eq[:], 0.0, OP.mult, OP.max), ["HOLDO", "HOLDE", "eq"], ["lo"])
+        tt(T.tx[:, 1::2], T.lo[:, 31:256:32], T.ewf[:, 1::2], OP.max, ["lo", "ewf"], ["txO"])
+        tt(T.tx[:, 0::2], T.lo[:, 271:384:16], T.ewf[:, 0::2], OP.max, ["lo", "ewf"], ["txE"])
+        cp(T.off[:], T.tx[:], ["txO", "txE"], ["off"])
+        for b in range(7, -1, -1):
+            cp(T.X[:].indirect(T.off[:, 2 * b:2 * b + 2]), T.nx[:, 32 * b:32 * b + 32], ["off", "nx"], ["X"])
+        act(T.RW[:, (SO - 1 - t) * 256:(SO - t) * 256], T.pR[:, 0:256], AF.Copy, ["pR"], ["RWs%d" % (SO - 1 - t)], ["pR"], bias=2048.0)
+        if not last:
+            act(T.RW2[:, (S2 - 1 - t) * 256:(S2 - t) * 256], T.pR[:, 0:256], AF.Copy, ["pR"], ["RW2s%d" % (S2 - 1 - t)], ["pR"], bias=2048.0)
+        if t == 0:
+            spread(T.LR1, "LR1", T.RW, "RW", SO - 16, 15, range(4, 8))
+        if t == 1:
+            spread(T.LR2, "LR2", T.RW2, "RW2", S2 + 16, 14, range(4, 7))
+        if not last:
+            for s in range(t):
+                if ((t + 1) % 3, s) in FOREIGN and ((t + 1) % 3, s) not in pushed:
+                    push_foreign((t + 1) % 3, s)()
+
+    dma("a", T.yr[:], T.RW[0:128:16, (SO - 6) * 256:(SO + 10) * 256], "dz", R=["RWs%d" % i for i in range(SO - 6, SO + 10)])
+    dma("s", T.yx[:], T.X[:, 0:4096], "dy", R=["X"])
+    for e in ("v", "a", "p", "q"):
+        g.wait_ge(T.sem[sem[e]], count[e])
+    g.wait_ge(T.sem.loc, loc[0])
+    g.wait_ge(T.sem.d2, 16)
+    g.wait_ge(T.sem.dz, 16)
+    g.wait_ge(T.sem.dy, 16)

@@ -1,4 +1,4 @@
-from concourse.mybir import AluOpType, AxisListType, ActivationFunctionType
+from concourse.mybir import AluOpType, ActivationFunctionType
 
 OP = AluOpType
 AF = ActivationFunctionType
@@ -7,9 +7,10 @@ SO = 21
 S2 = 5
 FOREIGN = [(k, s) for k in range(3) for s in range(STEPS - 1) if any(t > s for t in (k, k + 3))]
 A_PIECES = [(208, 32)]
-PIECES = [(0, 32), (208, 32), (32, 32), (64, 32), (96, 32), (128, 32), (160, 32), (192, 16), (240, 16)]
-BANKS = ["pD0", "pD1", "pD2", "pD3", "pL", "pR"]
-SCORE_AT = {4: 0, 6: 1, 8: 2}
+PIECES = [(0, 32), (32, 32), (208, 32), (64, 32), (96, 32), (128, 32), (160, 32), (192, 16), (240, 16)]
+BANKS = ["pD0", "pD1", "pL", "pR", "pD2", "pD3"]
+YEXP_AT = {0: [2], 1: [3], 2: [4], 3: [5], 4: [6], 5: [7], 6: [8]}
+SCORE_AT = {5: 0, 7: 1, 8: 2}
 
 F4, B2, F2, I4, U2 = "float32", "bfloat16", "float16", "int32", "uint16"
 SCRATCH = {}
@@ -19,16 +20,16 @@ for _n, _w, _d in [
         ("one", 512, B2), ("I16", 128, F2), ("KD", 128, F2), ("OD", 128, F2), ("AD", 128, F2), ("B16", 128, F2),
         ("IB", 128, B2), ("NI", 128, B2), ("PI", 128, B2), ("MI", 128, B2), ("ip", 1, I4), ("ipg", 1, I4), ("ipm", 1, I4),
         ("inn", 128, I4), ("ig", 128, I4), ("iL", 128, I4), ("iU", 128, I4), ("i32", 32, I4), ("i16", 16, I4), ("i1", 16, I4),
-        ("iq", 256, I4), ("i24", 24, I4), ("in3", 384, I4), ("colU", 16, F4), ("colL", 16, F4), ("pc", 1, F4), ("pg", 1, F4),
+        ("iq", 128, I4), ("i12", 12, I4), ("in3", 192, I4), ("colU", 16, F4), ("colL", 16, F4), ("pc", 1, F4), ("pg", 1, F4),
         ("pm", 1, F4), ("pm16", 1, F4), ("is0", 1, F4), ("is1", 1, F4), ("dmE", 1, F4), ("dmO", 1, F4), ("wf", 1, F4), ("wg", 1, F4),
         ("wh", 1, F4), ("kf", 1, F4), ("kg", 1, F4), ("kh", 1, F4), ("odd", 1, F4), ("cc0", 1, F4), ("acc", 1, F4),
-        ("cntf", 1, F4), ("cnti", 1, I4), ("cnta", 1, I4), ("LANE", 32, F2), ("C4", 32, B2), ("MC", 256, F2), ("RS", 256, F4),
-        ("HOLD", 384, F4), ("MK", 384, F4), ("CL", 24, U2), ("OH", 16, B2), ("ELI", 32, U2), ("EL", 16 * STEPS, U2),
+        ("cntf", 1, F4), ("cnti", 1, I4), ("cnta", 1, I4), ("jk", 32, B2), ("LANE", 32, F2), ("C4", 32, B2), ("MC", 128, F2),
+        ("RS", 128, F4), ("HOLD", 192, F4), ("MK", 192, F2), ("CL", 12, U2), ("OH", 16, B2), ("ELI", 32, U2), ("EL", 16 * STEPS, U2),
         ("Ga", 512, B2), ("xi", 32, I4), ("xj", 32, I4), ("RL", 32, U2), ("flg", 32, B2), ("PQ", 512, F2), ("PL", 32, U2),
         ("pr", 256, I4), ("sh", 256, I4), ("ci", 256, I4), ("cj", 256, I4), ("cl", 256, U2), ("c16", 256, F2), ("XPQ", 512, B2),
         ("sg", 256, B2), ("YT", 256, B2), ("G", 4096, B2), ("mn", 256, F4), ("ki", 16, I4), ("kj", 16, I4), ("ML", 16, U2),
-        ("z", 256, F2), ("ewf", 16, F4), ("e16", 16 * STEPS, F2), ("ER", 384, F4), ("eq", 384, B2), ("lo", 384, F4),
-        ("tx", 16, F4), ("off", 16, U2), ("XE", 256, B2), ("nx", 256, I4),
+        ("z", 256, F2), ("ewf", 16, F4), ("e16", 16 * STEPS, F2), ("EX0", 192, F4), ("EX1", 192, F4), ("eq", 384, B2),
+        ("lo", 384, F4), ("tx", 16, F4), ("off", 16, U2), ("XE", 256, B2), ("nx", 256, I4),
         ("LR0", 256, F2), ("LR1", 256, F2), ("LR2", 256, F2)] + [("LE%d%d" % ks, 16, F2) for ks in FOREIGN]:
     SCRATCH[_n] = ("sbuf", [128, _w], _d)
 SCRATCH["MA"] = ("sbuf", [128, 256, 16], B2)
@@ -161,32 +162,31 @@ def rank_program(g, core, T, topo):
     for k in range(3):
         send(k, T["LR%d" % k][:], T.r16[:], "ar%d" % k, ["r16"])
         arrived(k, "ar%d" % k, "LR%d" % k)
-    iota("iq", [[0, 16], [1, 16]], 0, 0)
+    iota("iq", [[0, 8], [1, 16]], 0, 0)
     op("v", lambda: V.memset(T.one[:], 1.0), W=["one"])
     for j in range(4):
         op("q", lambda: g.affine_select(T.E[:, 512 * j:512 * j + 512], T.one[:], [[-1, 32], [0, 16]], OP.is_equal, 0.0, -32 * j, 1), ["one"], ["E%d" % j])
-    iota("in3", [[0, 8], [1, 32]], 0, 0, (0, 256))
-    iota("in3", [[0, 8], [1, 16]], 16, 0, (256, 384))
-    iota("i24", [[2, 8], [0, 2]], 1, 0, (0, 16))
-    iota("i24", [[2, 8]], 0, 0, (16, 24))
+    iota("in3", [[0, 4], [1, 32]], 0, 0, (0, 128))
+    iota("in3", [[0, 4], [1, 16]], 16, 0, (128, 192))
+    iota("i12", [[2, 4], [0, 2]], 1, 0, (0, 8))
+    iota("i12", [[2, 4]], 0, 0, (8, 12))
 
-    D = [T.pD0, T.pD1, T.pD2, T.pD3]
     dn = [0]
+    spread_banks = ["pD0", "pD1", "pD2", "pD3"]
 
     def spread(src, key, buf, bkey, slot, ages, pairs, copier="a"):
         for j in pairs:
             w = min(2, ages - 2 * j)
-            d = dn[0] % 4
+            bk = spread_banks[dn[0] % len(spread_banks)]
             dn[0] += 1
-            bk = "pD%d" % d
-            op("p", [mm(D[d][:, 256 * i:256 * i + 256], blk(T.U, 2 * j + i), src[:], True, True) for i in range(w)],
+            op("p", [mm(T[bk][:, 256 * i:256 * i + 256], blk(T.U, 2 * j + i), src[:], True, True) for i in range(w)],
                [key] + ["U%d" % (2 * j + i) for i in range(w)], [bk], [bk])
             o = buf[:, (slot + 2 * j) * 256:(slot + 2 * j + w) * 256]
             ws = [bkey + "s%d" % (slot + 2 * j + i) for i in range(w)]
             if copier == "v":
-                ts(o, D[d][:, 0:256 * w], 2048.0, OP.add, [bk], ws, B=[bk])
+                ts(o, T[bk][:, 0:256 * w], 2048.0, OP.add, [bk], ws, B=[bk])
             else:
-                act(o, D[d][:, 0:256 * w], AF.Copy, [bk], ws, [bk], bias=2048.0)
+                act(o, T[bk][:, 0:256 * w], AF.Copy, [bk], ws, [bk], bias=2048.0)
 
     spread(T.r16, "r16", T.RW, "RW", SO, 16, range(8))
     dma("s", T.RW2[:, S2 * 256:(S2 + 14) * 256], T.RW[:, SO * 256:(SO + 14) * 256], "d2",
@@ -230,19 +230,19 @@ def rank_program(g, core, T, topo):
             ts(T.dmO[:], T.pm[:], 4112.0, OP.add, ["pm"], ["dmO"])
             ts(T.RS[:], T.iq[:], 0.0, OP.is_equal, ["iq"], ["RS"], 1.0e9, OP.mult)
             ts(T.B16[:], T.ig[:], T.pg[:], OP.is_equal, ["ig", "pg"], ["B16"])
-            ts(T.HOLD[:, 0:256], T.in3[:, 0:256], 0.0, OP.is_gt, ["in3"], ["HOLDO"])
-            ts(T.HOLD[:, 256:384], T.in3[:, 256:384], 16.0, OP.is_gt, ["in3"], ["HOLDE"])
+            ts(T.HOLD[:, 0:128], T.in3[:, 0:128], 0.0, OP.is_gt, ["in3"], ["HOLDO"])
+            ts(T.HOLD[:, 128:192], T.in3[:, 128:192], 16.0, OP.is_gt, ["in3"], ["HOLDE"])
             ts(T.MK[:], T.in3[:], T.pm16[:], OP.is_ge, ["in3", "pm16"], ["MK"], 8192.0, OP.mult)
-            ts(T.HOLD[:, 31:256:32], T.in3[:, 31:256:32], 0.0, OP.mult, ["in3", "dmO"], ["HOLDO"], T.dmO[:], OP.add)
-            ts(T.HOLD[:, 271:384:16], T.in3[:, 271:384:16], 0.0, OP.mult, ["in3", "dmE"], ["HOLDE"], T.dmE[:], OP.add)
+            ts(T.HOLD[:, 31:128:32], T.in3[:, 31:128:32], 0.0, OP.mult, ["in3", "dmO"], ["HOLDO"], T.dmO[:], OP.add)
+            ts(T.HOLD[:, 143:192:16], T.in3[:, 143:192:16], 0.0, OP.mult, ["in3", "dmE"], ["HOLDE"], T.dmE[:], OP.add)
             ts(T.MK[:], T.MK[:], 2048.0, OP.add, ["MK"], ["MK"])
-            cp(T.CL[:], T.i24[:], ["i24"], ["CL"])
+            cp(T.CL[:], T.i12[:], ["i12"], ["CL"])
             ts(T.OH[:], T.i1[:], T.pm[:], OP.is_equal, ["i1", "pm"], ["OH"])
 
     def el(s):
         if s >= 0:
-            return T.EL[:, 16 * s:16 * s + 16], "EL%d" % s
-        return (T.ELI[:, 0:16] if s == -1 else T.ELI[:, 16:32]), "ELI"
+            return T.EL[:, 16 * s:16 * s + 16], ["EL%dh%d" % (s, h) for h in range(2)]
+        return (T.ELI[:, 0:16] if s == -1 else T.ELI[:, 16:32]), ["ELI"]
 
     Xw = T.X[:, 0:4096]
     pushed = set()
@@ -259,78 +259,97 @@ def rank_program(g, core, T, topo):
     def pkey(name, l0, n):
         return ["%s%d" % (name, c) for c in range(l0 // 16, (l0 + n) // 16)]
 
+    two = [(h, slice(16 * h, 16 * h + 16)) for h in range(2)]
+    half = [(h, slice(128 * h, 128 * h + 128)) for h in range(2)]
+    eight = [slice(8 * h, 8 * h + 8) for h in range(2)]
+    RB, NB = ["pR", "pL"], ["pD2", "pD3"]
+    KB, EB = [("pS", 0), ("pA", 256)], [("pS", 256), ("pA", 128)]
+
     for t in range(STEPS):
         k = t % 3
         last = t == STEPS - 1
         la, lka = el(t - 1)
         lb, lkb = el(t - 2)
-        put = None
-        if t > 0 and (k, t - 1) not in pushed:
-            put = push_foreign(k, t - 1)
-        cp(T.Ga[:, 0:256], Xw.indirect(la), ["X", lka], ["Ga0"])
+        put = push_foreign(k, t - 1) if t > 0 else None
+        cp(T.Ga[:, 0:256], Xw.indirect(la), ["X"] + lka, ["Ga0"])
         if t == 0:
-            cp(T.Ga[:, 256:512], Xw.indirect(lb), ["X", lkb], ["Ga1"])
+            cp(T.Ga[:, 256:512], Xw.indirect(lb), ["X"] + lkb, ["Ga1"])
             spread(T.LR0, "LR0", T.RW, "RW", SO + 16, 16, range(4))
             constants(0)
         else:
-            act(T.Ga[:, 256:512], Xw.indirect(lb), AF.Copy, ["X", lkb], ["Ga1"])
-        if put:
+            act(T.Ga[:, 256:512], Xw.indirect(lb), AF.Copy, ["X"] + lkb, ["Ga1"])
             put()
         ms = [mm(T.pA[:, 0:32], T.I16[:], T.LANE[:], True, False)]
         if k == 1:
             ms.append(mm(T.pA[:, 0:32], T.I16[:], T.C4[:], False, False))
         op("p", ms, ["I16", "LANE", "C4"], ["pA"], ["pA"])
         op("p", [mm(T.pA[:, 0:32], blk(T.WD, q), T.Ga[:, q::16], False, q == 15) for q in range(16)], ["WD", "Ga0", "Ga1"], ["pA"], ["pA"])
-        cp(T.xi[:], T.pA[:, 0:32], ["pA"], ["xi"], ["pA"])
-        ts(T.xj[:], T.xi[:], 8191, OP.bitwise_and, ["xi"], ["xj"])
-        cp(T.RL[:], T.xj[:], ["xj"], ["RL"])
+        for h, w in two:
+            cp(T.xi[:, w], T.pA[:, w], ["pA"], ["xi%d" % h], ["pA"])
+        for h, w in two:
+            ts(T.xj[:, w], T.xi[:, w], 8191, OP.bitwise_and, ["xi%d" % h], ["xj%d" % h])
+        for h, w in two:
+            cp(T.RL[:, w], T.xj[:, w], ["xj%d" % h], ["RL%d" % h])
         if t == 0:
             spread(T.LR0, "LR0", T.RW, "RW", SO + 16, 16, (4, 5))
             spread(T.LR0, "LR0", T.RW, "RW", SO + 16, 16, (6, 7), "v")
             op("v", lambda: V.memset(T.C4[:], 4096.0), W=["C4"])
         buf, rk, w0 = [(T.RW, "RW", SO - t), (T.RW, "RW", SO - 16 - t), (T.RW2, "RW2", S2 - t)][k]
-        ts(T.PQ[:], buf[:, w0 * 256:(w0 + 32) * 256].indirect(T.RL[:]), -2048.0, OP.add, ["RL"] + [rk + "s%d" % i for i in range(w0, w0 + 32)], ["PQ"])
+        slots = [rk + "s%d" % i for i in range(w0, w0 + 32)]
+        ts(T.PQ[:], buf[:, w0 * 256:(w0 + 32) * 256].indirect(T.RL[:]), -2048.0, OP.add, ["RL0", "RL1"] + slots + [x + "h" for x in slots], ["PQ"])
         op("p", [mm(T.pA[:, 64:96], blk(T.L, q), T.PQ[:, q::16], q == 0, q == 15) for q in range(16)], ["PQ", "L"], ["pA"], ["pA"])
         op("p", [mm(T.pL[:, 0:256], T.KD[:], T.PQ[:, 0:256], True, False), mm(T.pL[:, 0:256], T.OD[:], T.PQ[:, 256:512], False, False),
                  mm(T.pL[:, 0:256], T.AD[:], T.one[:, 0:256], False, True)], ["PQ", "KD", "OD", "AD", "one"], ["pL"], ["pL"])
-        tt(T.pr[:], T.PQ[:, 0:256], T.PQ[:, 256:512], OP.mult, ["PQ"], ["pr"])
+        for h, w in half:
+            tt(T.pr[:, w], T.PQ[:, w], T.PQ[:, 256 + 128 * h:384 + 128 * h], OP.mult, ["PQ"], ["pr%d" % h])
         if not last:
-            ts(T.flg[:], T.xj[:], 4096.0, OP.is_lt if k == 1 else OP.is_ge, ["xj"], ["flg"])
+            ts(T.flg[:], T.xj[:], 4096.0, OP.is_lt if k == 1 else OP.is_ge, ["xj0", "xj1"], ["flg"])
         ts(T.PL[:], T.pA[:, 64:96], 0.0625, OP.mult, ["pA"], ["PL"], 2048.0, OP.add, B=["pA"])
-        ts(T.sh[:], T.pr[:], 5, OP.arith_shift_right, ["pr"], ["sh"])
-        tt(T.ci[:], T.sh[:], T.pL[:, 0:256], OP.add, ["sh", "pL"], ["ci"], ["pL"])
-        ts(T.cj[:], T.ci[:], 4095, OP.bitwise_and, ["ci"], ["cj"])
-        cp(T.cl[:], T.cj[:], ["cj"], ["cl"])
+        for h, w in half:
+            ts(T.sh[:, w], T.pr[:, w], 5, OP.arith_shift_right, ["pr%d" % h], ["sh%d" % h])
+        for h, w in half:
+            tt(T.ci[:, w], T.sh[:, w], T.pL[:, w], OP.add, ["sh%d" % h, "pL"], ["ci%d" % h], ["pL"])
+        for h, w in half:
+            ts(T.cj[:, w], T.ci[:, w], 4095, OP.bitwise_and, ["ci%d" % h], ["cj%d" % h])
+        for h, w in half:
+            cp(T.cl[:, w], T.cj[:, w], ["cj%d" % h], ["cl%d" % h])
         if t == 0:
             constants(1)
         act(T.XPQ[:], Xw.indirect(T.PL[:]), AF.Copy, ["X", "PL"], ["XPQ"])
         op("p", [mm(T.pS[:, 0:256], T.IB[:], T.XPQ[:, 0:256], True, False), mm(T.pS[:, 0:256], T.IB[:], T.XPQ[:, 256:512], False, True)],
            ["XPQ", "IB"], ["pS"], ["pS"])
-        act(T.sg[:], T.pS[:, 0:256], AF.Sign, ["pS"], ["sg"], ["pS"], bias=-255.5)
-        ms = []
-        for h in range(2):
-            o = T.pS[:, 256 + 128 * h:384 + 128 * h]
-            ms += [mm(o, T.XPQ[:, 128 * h:128 * h + 128], T.NI[:], True, False),
-                   mm(o, T.XPQ[:, 256 + 128 * h:384 + 128 * h], T.NI[:], False, False),
-                   mm(o, T.sg[:, 128 * h:128 * h + 128], T.PI[:], False, True)]
-        op("p", ms, ["XPQ", "sg", "NI", "PI"], ["pS"], ["pS"])
-        act(T.YT[:], T.pS[:, 256:512], AF.Copy, ["pS"], ["YT"], ["pS"], bias=128.0)
+        for h, w in half:
+            o = T[NB[h]][:, 0:128]
+            op("p", [mm(o, T.XPQ[:, w], T.NI[:], True, False), mm(o, T.XPQ[:, 256 + 128 * h:384 + 128 * h], T.NI[:], False, False)],
+               ["XPQ", "NI"], [NB[h]], [NB[h]])
+        for h, w in half:
+            act(T.sg[:, w], T.pS[:, w], AF.Sign, ["pS"], ["sg%d" % h], ["pS"], bias=-255.5)
+            op("p", mm(T[NB[h]][:, 0:128], T.sg[:, w], T.PI[:], False, True), ["sg%d" % h, "PI"], [NB[h]], [NB[h]])
+        for h, w in half:
+            act(T.YT[:, w], T[NB[h]][:, 0:128], AF.Copy, [NB[h]], ["YT%d" % h], [NB[h]], bias=128.0)
+        if not last:
+            op("p", mm(T.pA[:, 160:192], T.one[:, 0:128], T.flg[:], True, True), ["one", "flg"], ["pA"], ["pA"])
+            op("a", lambda: A.activation(T.jk[:], T.pA[:, 160:192], AF.Copy, accum_out=T.cntf[:]), ["pA"], ["jk", "cntf"], ["pA"])
         for l0, n in PIECES:
             o, i = T.G[:, 16 * l0:16 * (l0 + n)], Xw.indirect(T.cl[:, l0:l0 + n])
             if (l0, n) in A_PIECES:
-                act(o, i, AF.Copy, ["X", "cl"], pkey("G", l0, n))
+                act(o, i, AF.Copy, ["X", "cl%d" % (l0 // 128)], pkey("G", l0, n))
             else:
-                cp(o, i, ["X", "cl"], pkey("G", l0, n))
+                cp(o, i, ["X", "cl%d" % (l0 // 128)], pkey("G", l0, n))
 
         def yexp(s):
             l0, n = PIECES[s]
             bk, h = BANKS[s % len(BANKS)], l0 % 128
             op("p", mm(T[bk][:, 0:16 * n], blk(T.YT, l0 // 128), T.E[:, 16 * h:16 * (h + n)], True, False),
-               ["YT"] + ["E%d" % j for j in range(h // 32, (h + n + 31) // 32)], [bk], [bk])
+               ["YT%d" % (l0 // 128)] + ["E%d" % j for j in range(h // 32, (h + n + 31) // 32)], [bk], [bk])
 
         def score(Q):
-            op("p", [mm(T.pS[:, 64 * Q:64 * Q + 64], blk(T.L, q), T.MA[:, 64 * Q + q:64 * Q + 64:16, :], False, Q == 3 and q == 15)
-                     for q in range(16)], ["L"] + pkey("MA", 64 * Q, 64), ["pS"], ["pS"])
+            kb, o = KB[Q // 2]
+            o += 64 * (Q % 2)
+            op("p", [mm(T[kb][:, o:o + 64], blk(T.L, q), T.MA[:, 64 * Q + q:64 * Q + 64:16, :], False, Q % 2 == 1 and q == 15)
+                     for q in range(16)], ["L"] + pkey("MA", 64 * Q, 64), [kb], [kb])
+        for kb, o in KB:
+            op("p", mm(T[kb][:, o:o + 128], T.I16[:], T.MC[:], True, False), ["I16", "MC"], [kb], [kb])
         yexp(0)
         yexp(1)
         for s, (l0, n) in enumerate(PIECES):
@@ -338,62 +357,128 @@ def rank_program(g, core, T, topo):
             d = T[bk][:, 0:16 * n]
             op("p", mm(d, T.IB[:], T.G[:, 16 * l0:16 * (l0 + n)], False, True), ["IB"] + pkey("G", l0, n), [bk], [bk])
             act(T.MA[:, l0:l0 + n, :], d, AF.Abs, [bk], pkey("MA", l0, n), [bk])
-            if s == 1:
-                for x in range(2, len(BANKS)):
-                    yexp(x)
-                op("p", mm(T.pS[:, 0:256], T.I16[:], T.MC[:], True, False), ["I16", "MC"], ["pS"], ["pS"])
-                if not last:
-                    op("p", mm(T.pA[:, 160:192], T.one[:, 0:128], T.flg[:], True, True), ["one", "flg"], ["pA"], ["pA"])
-            if s >= 2 and s - 2 + len(BANKS) < len(PIECES):
-                yexp(s - 2 + len(BANKS))
+            for x in YEXP_AT.get(s, ()):
+                yexp(x)
             if s in SCORE_AT:
                 score(SCORE_AT[s])
         score(3)
-        op("p", [mm(T.pL[:, 0:256], T.IB[:], T.XPQ[:, 0:256], True, False), mm(T.pL[:, 0:256], T.IB[:], T.XPQ[:, 256:512], False, False),
-                 mm(T.pL[:, 0:256], T.MI[:], T.sg[:], False, False)], ["IB", "MI", "XPQ", "sg"], ["pL"], ["pL"])
         if t == 0:
             constants(2)
-        ts(T.c16[:], T.cj[:], -2048.0, OP.add, ["cj"], ["c16"])
-        if not last:
-            op("v", lambda: V.tensor_reduce(T.cntf[:], T.pA[:, 160:192], AxisListType.X, OP.add), ["pA"], ["cntf"], ["pA"])
-            cp(T.cnti[:], T.cntf[:], ["cntf"], ["cnti"])
-            ts(T.cnta[:], T.cnti[:], 63, OP.bitwise_and, ["cnti"], ["cnta"])
-            tt(T.acc[:], T.cnta[:], T.cc0[:], OP.add, ["cnta", "cc0"], ["acc"])
-            ts(T.AD[:], T.I16[:], T.acc[:], OP.mult, ["I16", "acc"], ["AD"])
+            spread_banks[:] = ["pD0", "pD1"]
+        for h, w in half:
+            ts(T.c16[:, w], T.cj[:, w], -2048.0, OP.add, ["cj%d" % h], ["c16%d" % h])
         if t == 0:
             spread(T.LR1, "LR1", T.RW, "RW", SO - 16, 15, range(4))
         if t == 1:
             spread(T.LR2, "LR2", T.RW2, "RW2", S2 + 16, 14, range(4))
-        op("v", lambda: V.tensor_tensor_scan(T.mn[:], T.RS[:], T.pS[:, 0:256], 0.0, OP.max, OP.min), ["RS", "pS"], ["mn"], ["pS"])
-        ts(T.ki[:], T.mn[:, 15::16], 32.0, OP.mult, ["mn"], ["ki"])
-        ts(T.kj[:], T.ki[:], 15, OP.bitwise_and, ["ki"], ["kj"])
-        cp(T.ML[:], T.kj[:], ["kj"], ["ML"])
-        tt(T.z[:], T.OH[:].indirect(T.ML[:]), T.c16[:], OP.mult, ["OH", "ML", "c16"], ["z"])
-        op("p", [mm(T.pA[:, 128:144], blk(T.L, q), T.z[:, q::16], q == 0, q == 15) for q in range(16)], ["L", "z"], ["pA"], ["pA"])
-        op("p", [mm(T.pR[:, 256 + 16 * b:272 + 16 * b], T.B16[:], T.z[:, 32 * b:32 * b + 16], True, True) for b in range(8)]
-           + [mm(T.pR[:, 0:256], T.B16[:], T.z[:], True, True)], ["B16", "z"], ["pR"], ["pR"])
-        en, ek = el(t)
-        ts(en, T.pA[:, 128:144], 2048.0, OP.add, ["pA"], [ek], B=["pA"])
-        ts(T.ewf[:], T.pA[:, 128:144], 2048.0, OP.add, ["pA"], ["ewf"], B=["pA"])
-        act(T.XE[:], Xw.indirect(en), AF.Copy, ["X", ek], ["XE"])
-        op("p", mm(T.pL[:, 0:256], T.IB[:], T.XE[:], False, True), ["IB", "XE"], ["pL"], ["pL"])
+
+        def scan(h):
+            kb, o = KB[h]
+            op("v", lambda: V.tensor_tensor_scan(T.mn[:, half[h][1]], T.RS[:], T[kb][:, o:o + 128], 0.0, OP.max, OP.min), ["RS", kb], ["mn%d" % h], [kb])
+
+        def ki(h):
+            ts(T.ki[:, eight[h]], T.mn[:, 128 * h + 15:128 * h + 128:16], 32.0, OP.mult, ["mn%d" % h], ["ki%d" % h])
+
+        def kj(h):
+            ts(T.kj[:, eight[h]], T.ki[:, eight[h]], 15, OP.bitwise_and, ["ki%d" % h], ["kj%d" % h])
+
+        def ml(h):
+            cp(T.ML[:, eight[h]], T.kj[:, eight[h]], ["kj%d" % h], ["ML%d" % h])
+
+        def choose(h):
+            w = half[h][1]
+            tt(T.z[:, w], T.OH[:].indirect(T.ML[:, eight[h]]), T.c16[:, w], OP.mult, ["OH", "ML%d" % h, "c16%d" % h], ["z%d" % h])
+            eb, o = EB[h]
+            op("p", [mm(T[eb][:, o:o + 8], blk(T.L, q), T.z[:, 128 * h + q:128 * h + 128:16], q == 0, q == 15) for q in range(16)], ["L", "z%d" % h], [eb], [eb])
+            rb = T[RB[h]]
+            op("p", [mm(rb[:, 0:192], T.I16[:], T.MK[:], True, False), mm(rb[:, 0:128], T.B16[:], T.z[:, w], False, False)]
+               + [mm(rb[:, 128 + 16 * b:144 + 16 * b], T.B16[:], T.z[:, 128 * h + 32 * b:128 * h + 32 * b + 16], False, b == 3) for b in range(4)]
+               + [mm(rb[:, 256:384], T.B16[:], T.z[:, w], True, True)], ["I16", "MK", "B16", "z%d" % h], [RB[h]], [RB[h]])
+
+        def oldsum(h):
+            o, w = T[NB[h]][:, 0:128], half[h][1]
+            op("p", [mm(o, T.IB[:], T.XPQ[:, w], True, False), mm(o, T.IB[:], T.XPQ[:, 256 + 128 * h:384 + 128 * h], False, False),
+                     mm(o, T.MI[:], T.sg[:, w], False, False)], ["IB", "MI", "XPQ", "sg%d" % h], [NB[h]], [NB[h]])
+
+        def lists(h):
+            eb, o = EB[h]
+            ts(T.EL[:, 16 * t + 8 * h:16 * t + 8 * h + 8], T[eb][:, o:o + 8], 2048.0, OP.add, [eb], ["EL%dh%d" % (t, h)], B=[eb])
+            ts(T.ewf[:, eight[h]], T[eb][:, o:o + 8], 2048.0, OP.add, [eb], ["ewf%d" % h], B=[eb])
+            if not last:
+                cp(T.e16[:, 16 * t + 8 * h:16 * t + 8 * h + 8], T[eb][:, o:o + 8], [eb], ["e16%d" % h], [eb])
+            ex = T["EX%d" % h]
+            act(ex[:], T.ewf[:, eight[h]].indirect(T.CL[:]), AF.Copy, ["ewf%d" % h, "CL"], ["EX%d" % h])
+
+        def old(h):
+            act(T.XE[:, half[h][1]], Xw.indirect(T.EL[:, 16 * t + 8 * h:16 * t + 8 * h + 8]), AF.Copy, ["X", "EL%dh%d" % (t, h)], ["XE%d" % h])
+            op("p", mm(T[NB[h]][:, 0:128], T.IB[:], T.XE[:, half[h][1]], False, True), ["IB", "XE%d" % h], [NB[h]], [NB[h]])
+
+        def nx(h):
+            ts(T.nx[:, half[h][1]], T[NB[h]][:, 0:128], 0.5, OP.mult, [NB[h]], ["nx%d" % h], -64.25, OP.add, B=[NB[h]])
+
+        def eq(h):
+            tt(T.eq[:, 192 * h:192 * h + 192], T["EX%d" % h][:], T[RB[h]][:, 0:192], OP.is_equal, ["EX%d" % h, RB[h]], ["eq%d" % h], [RB[h]])
+
+        def lo(h):
+            w = slice(192 * h, 192 * h + 192)
+            op("v", lambda: V.tensor_tensor_scan(T.lo[:, w], T.HOLD[:], T.eq[:, w], 0.0, OP.mult, OP.max), ["HOLDO", "HOLDE", "eq%d" % h], ["lo%d" % h])
+
+        def tx(h):
+            tt(T.tx[:, 8 * h + 1:8 * h + 8:2], T.lo[:, 192 * h + 31:192 * h + 128:32], T.ewf[:, 8 * h + 1:8 * h + 8:2], OP.max, ["lo%d" % h, "ewf%d" % h], ["txO%d" % h])
+            tt(T.tx[:, 8 * h:8 * h + 8:2], T.lo[:, 192 * h + 143:192 * h + 192:16], T.ewf[:, 8 * h:8 * h + 8:2], OP.max, ["lo%d" % h, "ewf%d" % h], ["txE%d" % h])
+
+        def off(h):
+            cp(T.off[:, eight[h]], T.tx[:, eight[h]], ["txO%d" % h, "txE%d" % h], ["off%d" % h])
+
+        def scatter(b):
+            cp(T.X[:].indirect(T.off[:, 2 * b:2 * b + 2]), T.nx[:, 32 * b:32 * b + 32], ["off%d" % (b // 4), "nx%d" % (b // 4)], ["X"])
+
+        scan(0)
         if not last:
-            cp(T.e16[:, 16 * t:16 * t + 16], T.pA[:, 128:144], ["pA"], ["e16%d" % t], ["pA"])
+            cp(T.cnti[:], T.cntf[:], ["cntf"], ["cnti"])
+        ki(0)
+        if not last:
+            ts(T.cnta[:], T.cnti[:], 63, OP.bitwise_and, ["cnti"], ["cnta"])
+        kj(0)
+        if not last:
+            tt(T.acc[:], T.cnta[:], T.cc0[:], OP.add, ["cnta", "cc0"], ["acc"])
+        ml(0)
+        choose(0)
+        scan(1)
+        if not last:
+            ts(T.AD[:], T.I16[:], T.acc[:], OP.mult, ["I16", "acc"], ["AD"])
+        ki(1)
+        kj(1)
+        ml(1)
+        choose(1)
+        oldsum(1)
+        oldsum(0)
+        lists(0)
+        lists(1)
+        if not last:
             for kk in sorted(range(3), key=lambda x: (x - t - 1) % 3):
                 if (kk, t) in FOREIGN:
-                    send(kk, T["LE%d%d" % (kk, t)][:], T.e16[:, 16 * t:16 * t + 16], "ae%d%d" % (kk, t), ["e16%d" % t])
-        tt(T.ER[:], T.pR[:, 0:384], T.MK[:], OP.add, ["pR", "MK"], ["ER"], ["pR"])
-        tt(T.eq[:], T.ewf[:].indirect(T.CL[:]), T.ER[:], OP.is_equal, ["ewf", "CL", "ER"], ["eq"])
-        ts(T.nx[:], T.pL[:, 0:256], 0.5, OP.mult, ["pL"], ["nx"], -64.25, OP.add, B=["pL"])
-        op("v", lambda: V.tensor_tensor_scan(T.lo[:], T.HOLD[:], T.eq[:], 0.0, OP.mult, OP.max), ["HOLDO", "HOLDE", "eq"], ["lo"])
-        tt(T.tx[:, 1::2], T.lo[:, 31:256:32], T.ewf[:, 1::2], OP.max, ["lo", "ewf"], ["txO"])
-        tt(T.tx[:, 0::2], T.lo[:, 271:384:16], T.ewf[:, 0::2], OP.max, ["lo", "ewf"], ["txE"])
-        cp(T.off[:], T.tx[:], ["txO", "txE"], ["off"])
-        for b in range(7, -1, -1):
-            cp(T.X[:].indirect(T.off[:, 2 * b:2 * b + 2]), T.nx[:, 32 * b:32 * b + 32], ["off", "nx"], ["X"])
-        act(T.RW[:, (SO - 1 - t) * 256:(SO - t) * 256], T.pR[:, 0:256], AF.Copy, ["pR"], ["RWs%d" % (SO - 1 - t)], ["pR"], bias=2048.0)
-        if not last:
-            act(T.RW2[:, (S2 - 1 - t) * 256:(S2 - t) * 256], T.pR[:, 0:256], AF.Copy, ["pR"], ["RW2s%d" % (S2 - 1 - t)], ["pR"], bias=2048.0)
+                    send(kk, T["LE%d%d" % (kk, t)][:], T.e16[:, 16 * t:16 * t + 16], "ae%d%d" % (kk, t), ["e160", "e161"])
+        old(1)
+        old(0)
+        eq(0)
+        eq(1)
+        lo(0)
+        lo(1)
+        tx(0)
+        tx(1)
+        nx(1)
+        off(1)
+        scatter(7)
+        off(0)
+        scatter(6)
+        nx(0)
+        for b in (5, 4, 3, 2, 1, 0):
+            scatter(b)
+        for h in range(2):
+            for buf, bkey, slot in [(T.RW, "RW", SO - 1 - t), (T.RW2, "RW2", S2 - 1 - t)][:1 if last else 2]:
+                act(buf[:, slot * 256 + 128 * h:slot * 256 + 128 * h + 128], T[RB[h]][:, 256:384], AF.Copy, [RB[h]],
+                    [bkey + "s%d%s" % (slot, "" if h else "h")], [RB[h]], bias=2048.0)
         if t == 0:
             spread(T.LR1, "LR1", T.RW, "RW", SO - 16, 15, range(4, 8))
         if t == 1:
@@ -403,7 +488,8 @@ def rank_program(g, core, T, topo):
                 if ((t + 1) % 3, s) in FOREIGN and ((t + 1) % 3, s) not in pushed:
                     push_foreign((t + 1) % 3, s)()
 
-    dma("a", T.yr[:], T.RW[0:128:16, (SO - 6) * 256:(SO + 10) * 256], "dz", R=["RWs%d" % i for i in range(SO - 6, SO + 10)])
+    slots = ["RWs%d" % i for i in range(SO - 6, SO + 10)]
+    dma("a", T.yr[:], T.RW[0:128:16, (SO - 6) * 256:(SO + 10) * 256], "dz", R=slots + [x + "h" for x in slots])
     dma("s", T.yx[:], T.X[:, 0:4096], "dy", R=["X"])
     for e in ("v", "a", "p", "q"):
         g.wait_ge(T.sem[sem[e]], count[e])

@@ -6,11 +6,17 @@ STEPS = 6
 SO = 21
 S2 = 5
 FOREIGN = [(k, s) for k in range(3) for s in range(STEPS - 1) if any(t > s for t in (k, k + 3))]
-A_PIECES = [(208, 32)]
-PIECES = [(0, 32), (32, 32), (208, 32), (64, 32), (96, 32), (128, 32), (160, 32), (192, 16), (240, 16)]
+A_PIECES = [(16, 32)]
+PIECES = [(224, 32), (192, 32), (16, 32), (160, 32), (128, 32), (96, 32), (64, 32), (48, 16), (0, 16)]
 BANKS = ["pD0", "pD1", "pL", "pR", "pD2", "pD3"]
 YEXP_AT = {0: [2], 1: [3], 2: [4], 3: [5], 4: [6], 5: [7], 6: [8]}
-SCORE_AT = {5: 0, 7: 1, 8: 2}
+SCORE_AT = {4: 3, 6: 2, 8: 1}
+TAIL = [("count", 0), ("c16", 0), ("scan", 1), ("ki", 1), ("c16", 1), ("count", 1), ("kj", 1), ("count", 2), ("ml", 1),
+        ("choose", 1), ("gl", 1), ("count", 3), ("scan", 0), ("ki", 0), ("gl2", 1), ("oldsum", 1), ("kj", 0), ("lists", 1),
+        ("ml", 0), ("gl", 0), ("old", 1), ("oldsum", 0), ("ex", 1), ("choose", 0), ("eq", 1), ("nx", 1), ("lo", 1),
+        ("lists", 0), ("tx", 1), ("gl2", 0), ("off", 1), ("ex", 0), ("scatter", 7), ("old", 0), ("eq", 0), ("scatter", 6),
+        ("lo", 0), ("scatter", 5), ("tx", 0), ("nx", 0), ("scatter", 4), ("off", 0), ("scatter", 3), ("scatter", 2),
+        ("scatter", 1), ("scatter", 0)]
 
 F4, B2, F2, I4, U2 = "float32", "bfloat16", "float16", "int32", "uint16"
 SCRATCH = {}
@@ -28,9 +34,9 @@ for _n, _w, _d in [
         ("Ga", 512, B2), ("xi", 32, I4), ("xj", 32, I4), ("RL", 32, U2), ("flg", 32, B2), ("PQ", 512, F2), ("PL", 32, U2),
         ("pr", 256, I4), ("sh", 256, I4), ("ci", 256, I4), ("cj", 256, I4), ("cl", 256, U2), ("c16", 256, F2), ("XPQ", 512, B2),
         ("sg", 256, B2), ("YT", 256, B2), ("G", 4096, B2), ("mn", 256, F4), ("ki", 16, I4), ("kj", 16, I4), ("ML", 16, U2),
-        ("z", 256, F2), ("ewf", 16, F4), ("e16", 16 * STEPS, F2), ("EX0", 192, F4), ("EX1", 192, F4), ("eq", 384, B2),
-        ("lo", 384, F4), ("tx", 16, F4), ("off", 16, U2), ("XE", 256, B2), ("nx", 256, I4),
-        ("LR0", 256, F2), ("LR1", 256, F2), ("LR2", 256, F2)] + [("LE%d%d" % ks, 16, F2) for ks in FOREIGN]:
+        ("LG", 16, I4), ("kl", 16, I4), ("GL", 16, U2), ("z", 256, F2), ("ewf", 16, F4), ("e16", 16 * STEPS, F2),
+        ("EX0", 192, F4), ("EX1", 192, F4), ("eq", 384, B2), ("lo", 384, F4), ("tx", 16, F4), ("off", 16, U2), ("XE", 256, B2),
+        ("nx", 256, I4), ("LR0", 256, F2), ("LR1", 256, F2), ("LR2", 256, F2)] + [("LE%d%d" % ks, 16, F2) for ks in FOREIGN]:
     SCRATCH[_n] = ("sbuf", [128, _w], _d)
 SCRATCH["MA"] = ("sbuf", [128, 256, 16], B2)
 for _n in ("pA", "pL", "pR", "pS", "pD0", "pD1", "pD2", "pD3"):
@@ -162,14 +168,6 @@ def rank_program(g, core, T, topo):
     for k in range(3):
         send(k, T["LR%d" % k][:], T.r16[:], "ar%d" % k, ["r16"])
         arrived(k, "ar%d" % k, "LR%d" % k)
-    iota("iq", [[0, 8], [1, 16]], 0, 0)
-    op("v", lambda: V.memset(T.one[:], 1.0), W=["one"])
-    for j in range(4):
-        op("q", lambda: g.affine_select(T.E[:, 512 * j:512 * j + 512], T.one[:], [[-1, 32], [0, 16]], OP.is_equal, 0.0, -32 * j, 1), ["one"], ["E%d" % j])
-    iota("in3", [[0, 4], [1, 32]], 0, 0, (0, 128))
-    iota("in3", [[0, 4], [1, 16]], 16, 0, (128, 192))
-    iota("i12", [[2, 4], [0, 2]], 1, 0, (0, 8))
-    iota("i12", [[2, 4]], 0, 0, (8, 12))
 
     dn = [0]
     spread_banks = ["pD0", "pD1", "pD2", "pD3"]
@@ -204,6 +202,14 @@ def rank_program(g, core, T, topo):
     ts(T.LANE[:], T.i32[:], T.pm[:], OP.add, ["i32", "pm"], ["LANE"])
     ts(T.ELI[:], T.pA[:, 64:96], 2048.0, OP.add, ["pA"], ["ELI"], B=["pA"])
     ts(T.WD[:], T.L[:], T.wf[:], OP.mult, ["L", "wf"] + ["L_%d" % q for q in range(15)], ["WD"])
+    op("v", lambda: V.memset(T.one[:], 1.0), W=["one"])
+    for j in (3, 2, 0, 1):
+        op("q", lambda: g.affine_select(T.E[:, 512 * j:512 * j + 512], T.one[:], [[-1, 32], [0, 16]], OP.is_equal, 0.0, -32 * j, 1), ["one"], ["E%d" % j])
+    iota("iq", [[0, 8], [1, 16]], 0, 0)
+    iota("in3", [[0, 4], [1, 32]], 0, 0, (0, 128))
+    iota("in3", [[0, 4], [1, 16]], 16, 0, (128, 192))
+    iota("i12", [[2, 4], [0, 2]], 1, 0, (0, 8))
+    iota("i12", [[2, 4]], 0, 0, (8, 12))
 
     def constants(part):
         if part == 0:
@@ -222,6 +228,7 @@ def rank_program(g, core, T, topo):
             ts(T.PI[:], T.I16[:], 128.0, OP.mult, ["I16"], ["PI"])
         elif part == 1:
             ts(T.MC[:], T.iq[:], 0.03125, OP.mult, ["iq"], ["MC"])
+            ts(T.LG[:], T.i16[:], T.pm[:], OP.add, ["i16", "pm"], ["LG"], 16.0, OP.mult)
             ts(T.MI[:], T.I16[:], -128.0, OP.mult, ["I16"], ["MI"])
         else:
             ts(T.ig[:], T.inn[:], 4, OP.arith_shift_right, ["inn"], ["ig"])
@@ -260,9 +267,11 @@ def rank_program(g, core, T, topo):
         return ["%s%d" % (name, c) for c in range(l0 // 16, (l0 + n) // 16)]
 
     two = [(h, slice(16 * h, 16 * h + 16)) for h in range(2)]
-    half = [(h, slice(128 * h, 128 * h + 128)) for h in range(2)]
+    hw = [slice(0, 128), slice(128, 256)]
+    half = [(1, hw[1]), (0, hw[0])]
     eight = [slice(8 * h, 8 * h + 8) for h in range(2)]
-    RB, NB = ["pR", "pL"], ["pD2", "pD3"]
+    DB = ["pD2", "pA"]
+    RB, NB = ["pL", "pR"], ["pD2", "pD3"]
     KB, EB = [("pS", 0), ("pA", 256)], [("pS", 256), ("pA", 128)]
 
     for t in range(STEPS):
@@ -296,15 +305,22 @@ def rank_program(g, core, T, topo):
             op("v", lambda: V.memset(T.C4[:], 4096.0), W=["C4"])
         buf, rk, w0 = [(T.RW, "RW", SO - t), (T.RW, "RW", SO - 16 - t), (T.RW2, "RW2", S2 - t)][k]
         slots = [rk + "s%d" % i for i in range(w0, w0 + 32)]
-        ts(T.PQ[:], buf[:, w0 * 256:(w0 + 32) * 256].indirect(T.RL[:]), -2048.0, OP.add, ["RL0", "RL1"] + slots + [x + "h" for x in slots], ["PQ"])
-        op("p", [mm(T.pA[:, 64:96], blk(T.L, q), T.PQ[:, q::16], q == 0, q == 15) for q in range(16)], ["PQ", "L"], ["pA"], ["pA"])
+        win = buf[:, w0 * 256:(w0 + 32) * 256]
+        for h, w in two:
+            ts(T.PQ[:, 256 * h:256 * h + 256], win.indirect(T.RL[:, w]), -2048.0, OP.add, ["RL%d" % h] + slots + [x + "h" for x in slots], ["PQ%d" % h])
+            op("p", [mm(T[DB[h]][:, 64:80], blk(T.L, q), T.PQ[:, 256 * h + q:256 * h + 256:16], q == 0, q == 15) for q in range(16)],
+               ["PQ%d" % h, "L"], [DB[h]], [DB[h]])
         op("p", [mm(T.pL[:, 0:256], T.KD[:], T.PQ[:, 0:256], True, False), mm(T.pL[:, 0:256], T.OD[:], T.PQ[:, 256:512], False, False),
-                 mm(T.pL[:, 0:256], T.AD[:], T.one[:, 0:256], False, True)], ["PQ", "KD", "OD", "AD", "one"], ["pL"], ["pL"])
+                 mm(T.pL[:, 0:256], T.AD[:], T.one[:, 0:256], False, True)], ["PQ0", "PQ1", "KD", "OD", "AD", "one"], ["pL"], ["pL"])
+
+        def names(h):
+            ts(T.PL[:, two[h][1]], T[DB[h]][:, 64:80], 0.0625, OP.mult, [DB[h]], ["PL%d" % h], 2048.0, OP.add, B=[DB[h]])
+        names(0)
         for h, w in half:
-            tt(T.pr[:, w], T.PQ[:, w], T.PQ[:, 256 + 128 * h:384 + 128 * h], OP.mult, ["PQ"], ["pr%d" % h])
+            tt(T.pr[:, w], T.PQ[:, w], T.PQ[:, 256 + 128 * h:384 + 128 * h], OP.mult, ["PQ0", "PQ1"], ["pr%d" % h])
         if not last:
             ts(T.flg[:], T.xj[:], 4096.0, OP.is_lt if k == 1 else OP.is_ge, ["xj0", "xj1"], ["flg"])
-        ts(T.PL[:], T.pA[:, 64:96], 0.0625, OP.mult, ["pA"], ["PL"], 2048.0, OP.add, B=["pA"])
+        names(1)
         for h, w in half:
             ts(T.sh[:, w], T.pr[:, w], 5, OP.arith_shift_right, ["pr%d" % h], ["sh%d" % h])
         for h, w in half:
@@ -315,13 +331,14 @@ def rank_program(g, core, T, topo):
             cp(T.cl[:, w], T.cj[:, w], ["cj%d" % h], ["cl%d" % h])
         if t == 0:
             constants(1)
-        act(T.XPQ[:], Xw.indirect(T.PL[:]), AF.Copy, ["X", "PL"], ["XPQ"])
+        for h, w in two:
+            act(T.XPQ[:, 256 * h:256 * h + 256], Xw.indirect(T.PL[:, w]), AF.Copy, ["X", "PL%d" % h], ["XPQ%d" % h])
         op("p", [mm(T.pS[:, 0:256], T.IB[:], T.XPQ[:, 0:256], True, False), mm(T.pS[:, 0:256], T.IB[:], T.XPQ[:, 256:512], False, True)],
-           ["XPQ", "IB"], ["pS"], ["pS"])
+           ["XPQ0", "XPQ1", "IB"], ["pS"], ["pS"])
         for h, w in half:
             o = T[NB[h]][:, 0:128]
             op("p", [mm(o, T.XPQ[:, w], T.NI[:], True, False), mm(o, T.XPQ[:, 256 + 128 * h:384 + 128 * h], T.NI[:], False, False)],
-               ["XPQ", "NI"], [NB[h]], [NB[h]])
+               ["XPQ0", "XPQ1", "NI"], [NB[h]], [NB[h]])
         for h, w in half:
             act(T.sg[:, w], T.pS[:, w], AF.Sign, ["pS"], ["sg%d" % h], ["pS"], bias=-255.5)
             op("p", mm(T[NB[h]][:, 0:128], T.sg[:, w], T.PI[:], False, True), ["sg%d" % h, "PI"], [NB[h]], [NB[h]])
@@ -346,7 +363,7 @@ def rank_program(g, core, T, topo):
         def score(Q):
             kb, o = KB[Q // 2]
             o += 64 * (Q % 2)
-            op("p", [mm(T[kb][:, o:o + 64], blk(T.L, q), T.MA[:, 64 * Q + q:64 * Q + 64:16, :], False, Q % 2 == 1 and q == 15)
+            op("p", [mm(T[kb][:, o:o + 64], blk(T.L, q), T.MA[:, 64 * Q + q:64 * Q + 64:16, :], False, Q % 2 == 0 and q == 15)
                      for q in range(16)], ["L"] + pkey("MA", 64 * Q, 64), [kb], [kb])
         for kb, o in KB:
             op("p", mm(T[kb][:, o:o + 128], T.I16[:], T.MC[:], True, False), ["I16", "MC"], [kb], [kb])
@@ -361,20 +378,28 @@ def rank_program(g, core, T, topo):
                 yexp(x)
             if s in SCORE_AT:
                 score(SCORE_AT[s])
-        score(3)
+        score(0)
         if t == 0:
             constants(2)
             spread_banks[:] = ["pD0", "pD1"]
-        for h, w in half:
-            ts(T.c16[:, w], T.cj[:, w], -2048.0, OP.add, ["cj%d" % h], ["c16%d" % h])
         if t == 0:
             spread(T.LR1, "LR1", T.RW, "RW", SO - 16, 15, range(4))
         if t == 1:
             spread(T.LR2, "LR2", T.RW2, "RW2", S2 + 16, 14, range(4))
 
+        def count_a(i):
+            if i == 0:
+                cp(T.cnti[:], T.cntf[:], ["cntf"], ["cnti"])
+            elif i == 1:
+                ts(T.cnta[:], T.cnti[:], 63, OP.bitwise_and, ["cnti"], ["cnta"])
+            elif i == 2:
+                tt(T.acc[:], T.cnta[:], T.cc0[:], OP.add, ["cnta", "cc0"], ["acc"])
+            else:
+                ts(T.AD[:], T.I16[:], T.acc[:], OP.mult, ["I16", "acc"], ["AD"])
+
         def scan(h):
             kb, o = KB[h]
-            op("v", lambda: V.tensor_tensor_scan(T.mn[:, half[h][1]], T.RS[:], T[kb][:, o:o + 128], 0.0, OP.max, OP.min), ["RS", kb], ["mn%d" % h], [kb])
+            op("v", lambda: V.tensor_tensor_scan(T.mn[:, hw[h]], T.RS[:], T[kb][:, o:o + 128], 0.0, OP.max, OP.min), ["RS", kb], ["mn%d" % h], [kb])
 
         def ki(h):
             ts(T.ki[:, eight[h]], T.mn[:, 128 * h + 15:128 * h + 128:16], 32.0, OP.mult, ["mn%d" % h], ["ki%d" % h])
@@ -385,8 +410,17 @@ def rank_program(g, core, T, topo):
         def ml(h):
             cp(T.ML[:, eight[h]], T.kj[:, eight[h]], ["kj%d" % h], ["ML%d" % h])
 
+        def c16(h):
+            ts(T.c16[:, hw[h]], T.cj[:, hw[h]], -2048.0, OP.add, ["cj%d" % h], ["c16%d" % h])
+
+        def gl(h):
+            tt(T.kl[:, eight[h]], T.kj[:, eight[h]], T.LG[:, eight[h]], OP.add, ["kj%d" % h, "LG"], ["kl%d" % h])
+
+        def gl2(h):
+            cp(T.GL[:, eight[h]], T.kl[:, eight[h]], ["kl%d" % h], ["GL%d" % h])
+
         def choose(h):
-            w = half[h][1]
+            w = hw[h]
             tt(T.z[:, w], T.OH[:].indirect(T.ML[:, eight[h]]), T.c16[:, w], OP.mult, ["OH", "ML%d" % h, "c16%d" % h], ["z%d" % h])
             eb, o = EB[h]
             op("p", [mm(T[eb][:, o:o + 8], blk(T.L, q), T.z[:, 128 * h + q:128 * h + 128:16], q == 0, q == 15) for q in range(16)], ["L", "z%d" % h], [eb], [eb])
@@ -396,9 +430,16 @@ def rank_program(g, core, T, topo):
                + [mm(rb[:, 256:384], T.B16[:], T.z[:, w], True, True)], ["I16", "MK", "B16", "z%d" % h], [RB[h]], [RB[h]])
 
         def oldsum(h):
-            o, w = T[NB[h]][:, 0:128], half[h][1]
+            o, w = T[NB[h]][:, 0:128], hw[h]
             op("p", [mm(o, T.IB[:], T.XPQ[:, w], True, False), mm(o, T.IB[:], T.XPQ[:, 256 + 128 * h:384 + 128 * h], False, False),
-                     mm(o, T.MI[:], T.sg[:, w], False, False)], ["IB", "MI", "XPQ", "sg%d" % h], [NB[h]], [NB[h]])
+                     mm(o, T.MI[:], T.sg[:, w], False, False)], ["IB", "MI", "XPQ0", "XPQ1", "sg%d" % h], [NB[h]], [NB[h]])
+
+        def old(h):
+            act(T.XE[:, hw[h]], T.G[:].indirect(T.GL[:, eight[h]]), AF.Copy, pkey("G", 0, 256) + ["GL%d" % h], ["XE%d" % h])
+            op("p", mm(T[NB[h]][:, 0:128], T.IB[:], T.XE[:, hw[h]], False, True), ["IB", "XE%d" % h], [NB[h]], [NB[h]])
+
+        def nx(h):
+            ts(T.nx[:, hw[h]], T[NB[h]][:, 0:128], 0.5, OP.mult, [NB[h]], ["nx%d" % h], -64.25, OP.add, B=[NB[h]])
 
         def lists(h):
             eb, o = EB[h]
@@ -406,15 +447,13 @@ def rank_program(g, core, T, topo):
             ts(T.ewf[:, eight[h]], T[eb][:, o:o + 8], 2048.0, OP.add, [eb], ["ewf%d" % h], B=[eb])
             if not last:
                 cp(T.e16[:, 16 * t + 8 * h:16 * t + 8 * h + 8], T[eb][:, o:o + 8], [eb], ["e16%d" % h], [eb])
-            ex = T["EX%d" % h]
-            act(ex[:], T.ewf[:, eight[h]].indirect(T.CL[:]), AF.Copy, ["ewf%d" % h, "CL"], ["EX%d" % h])
+                if h == 0:
+                    for kk in sorted(range(3), key=lambda x: (x - t - 1) % 3):
+                        if (kk, t) in FOREIGN:
+                            send(kk, T["LE%d%d" % (kk, t)][:], T.e16[:, 16 * t:16 * t + 16], "ae%d%d" % (kk, t), ["e160", "e161"])
 
-        def old(h):
-            act(T.XE[:, half[h][1]], Xw.indirect(T.EL[:, 16 * t + 8 * h:16 * t + 8 * h + 8]), AF.Copy, ["X", "EL%dh%d" % (t, h)], ["XE%d" % h])
-            op("p", mm(T[NB[h]][:, 0:128], T.IB[:], T.XE[:, half[h][1]], False, True), ["IB", "XE%d" % h], [NB[h]], [NB[h]])
-
-        def nx(h):
-            ts(T.nx[:, half[h][1]], T[NB[h]][:, 0:128], 0.5, OP.mult, [NB[h]], ["nx%d" % h], -64.25, OP.add, B=[NB[h]])
+        def ex(h):
+            act(T["EX%d" % h][:], T.ewf[:, eight[h]].indirect(T.CL[:]), AF.Copy, ["ewf%d" % h, "CL"], ["EX%d" % h])
 
         def eq(h):
             tt(T.eq[:, 192 * h:192 * h + 192], T["EX%d" % h][:], T[RB[h]][:, 0:192], OP.is_equal, ["EX%d" % h, RB[h]], ["eq%d" % h], [RB[h]])
@@ -433,48 +472,11 @@ def rank_program(g, core, T, topo):
         def scatter(b):
             cp(T.X[:].indirect(T.off[:, 2 * b:2 * b + 2]), T.nx[:, 32 * b:32 * b + 32], ["off%d" % (b // 4), "nx%d" % (b // 4)], ["X"])
 
-        scan(0)
-        if not last:
-            cp(T.cnti[:], T.cntf[:], ["cntf"], ["cnti"])
-        ki(0)
-        if not last:
-            ts(T.cnta[:], T.cnti[:], 63, OP.bitwise_and, ["cnti"], ["cnta"])
-        kj(0)
-        if not last:
-            tt(T.acc[:], T.cnta[:], T.cc0[:], OP.add, ["cnta", "cc0"], ["acc"])
-        ml(0)
-        choose(0)
-        scan(1)
-        if not last:
-            ts(T.AD[:], T.I16[:], T.acc[:], OP.mult, ["I16", "acc"], ["AD"])
-        ki(1)
-        kj(1)
-        ml(1)
-        choose(1)
-        oldsum(1)
-        oldsum(0)
-        lists(0)
-        lists(1)
-        if not last:
-            for kk in sorted(range(3), key=lambda x: (x - t - 1) % 3):
-                if (kk, t) in FOREIGN:
-                    send(kk, T["LE%d%d" % (kk, t)][:], T.e16[:, 16 * t:16 * t + 16], "ae%d%d" % (kk, t), ["e160", "e161"])
-        old(1)
-        old(0)
-        eq(0)
-        eq(1)
-        lo(0)
-        lo(1)
-        tx(0)
-        tx(1)
-        nx(1)
-        off(1)
-        scatter(7)
-        off(0)
-        scatter(6)
-        nx(0)
-        for b in (5, 4, 3, 2, 1, 0):
-            scatter(b)
+        parts = {"count": count_a, "scan": scan, "ki": ki, "kj": kj, "ml": ml, "c16": c16, "gl": gl, "gl2": gl2, "choose": choose,
+                 "oldsum": oldsum, "old": old, "nx": nx, "lists": lists, "ex": ex, "eq": eq, "lo": lo, "tx": tx, "off": off, "scatter": scatter}
+        for name, h in TAIL:
+            if not (last and name == "count"):
+                parts[name](h)
         for h in range(2):
             for buf, bkey, slot in [(T.RW, "RW", SO - 1 - t), (T.RW2, "RW2", S2 - 1 - t)][:1 if last else 2]:
                 act(buf[:, slot * 256 + 128 * h:slot * 256 + 128 * h + 128], T[RB[h]][:, 256:384], AF.Copy, [RB[h]],

from concourse.mybir import AluOpType, ActivationFunctionType

OP = AluOpType
AF = ActivationFunctionType
STEPS = 6
SO = 21
S2 = 5
FOREIGN = [(k, s) for k in range(3) for s in range(STEPS - 1) if any(t > s for t in (k, k + 3))]
A_PIECES = [(16, 32)]
PIECES = [(224, 32), (192, 32), (16, 32), (160, 32), (128, 32), (96, 32), (64, 32), (48, 16), (0, 16)]
BANKS = ["pD0", "pD1", "pL", "pR", "pD2", "pD3"]
YEXP_AT = {0: [2], 1: [3], 2: [4], 3: [5], 4: [6], 5: [7], 6: [8]}
SCORE_AT = {4: 3, 6: 2, 8: 1}
TAIL = [("count", 0), ("c16", 0), ("scan", 1), ("ki", 1), ("c16", 1), ("count", 1), ("kj", 1), ("count", 2), ("ml", 1),
        ("choose", 1), ("gl", 1), ("count", 3), ("scan", 0), ("ki", 0), ("gl2", 1), ("oldsum", 1), ("kj", 0), ("lists", 1),
        ("ml", 0), ("gl", 0), ("old", 1), ("oldsum", 0), ("ex", 1), ("choose", 0), ("eq", 1), ("nx", 1), ("lo", 1),
        ("lists", 0), ("tx", 1), ("gl2", 0), ("off", 1), ("ex", 0), ("scatter", 7), ("old", 0), ("eq", 0), ("scatter", 6),
        ("lo", 0), ("scatter", 5), ("tx", 0), ("nx", 0), ("scatter", 4), ("off", 0), ("scatter", 3), ("scatter", 2),
        ("scatter", 1), ("scatter", 0)]

F4, B2, F2, I4, U2 = "float32", "bfloat16", "float16", "int32", "uint16"
SCRATCH = {}
for _n, _w, _d in [
        ("X", 4128, B2), ("RW", 53 * 256, F4), ("RW2", 37 * 256, F4), ("ri", 256, I4), ("r16", 256, F2), ("zz", 512, F2),
        ("wti", 1, I4), ("kpi", 1, I4), ("kpb", 1, I4), ("U", 2048, F2), ("L", 2048, F2), ("WD", 2048, B2), ("E", 2048, B2),
        ("one", 512, B2), ("I16", 128, F2), ("KD", 128, F2), ("OD", 128, F2), ("AD", 128, F2), ("B16", 128, F2),
        ("IB", 128, B2), ("NI", 128, B2), ("PI", 128, B2), ("MI", 128, B2), ("ip", 1, I4), ("ipg", 1, I4), ("ipm", 1, I4),
        ("inn", 128, I4), ("ig", 128, I4), ("iL", 128, I4), ("iU", 128, I4), ("i32", 32, I4), ("i16", 16, I4), ("i1", 16, I4),
        ("iq", 128, I4), ("i12", 12, I4), ("in3", 192, I4), ("colU", 16, F4), ("colL", 16, F4), ("pc", 1, F4), ("pg", 1, F4),
        ("pm", 1, F4), ("pm16", 1, F4), ("is0", 1, F4), ("is1", 1, F4), ("dmE", 1, F4), ("dmO", 1, F4), ("wf", 1, F4), ("wg", 1, F4),
        ("wh", 1, F4), ("kf", 1, F4), ("kg", 1, F4), ("kh", 1, F4), ("odd", 1, F4), ("cc0", 1, F4), ("acc", 1, F4),
        ("cntf", 1, F4), ("cnti", 1, I4), ("cnta", 1, I4), ("jk", 32, B2), ("LANE", 32, F2), ("C4", 32, B2), ("MC", 128, F2),
        ("RS", 128, F4), ("HOLD", 192, F4), ("MK", 192, F2), ("CL", 12, U2), ("OH", 16, B2), ("ELI", 32, U2), ("EL", 16 * STEPS, U2),
        ("Ga", 512, B2), ("xi", 32, I4), ("xj", 32, I4), ("RL", 32, U2), ("flg", 32, B2), ("PQ", 512, F2), ("PL", 32, U2),
        ("pr", 256, I4), ("sh", 256, I4), ("ci", 256, I4), ("cj", 256, I4), ("cl", 256, U2), ("c16", 256, F2), ("XPQ", 512, B2),
        ("sg", 256, B2), ("YT", 256, B2), ("G", 4096, B2), ("mn", 256, F4), ("ki", 16, I4), ("kj", 16, I4), ("ML", 16, U2),
        ("LG", 16, I4), ("kl", 16, I4), ("GL", 16, U2), ("z", 256, F2), ("ewf", 16, F4), ("e16", 16 * STEPS, F2),
        ("EX0", 192, F4), ("EX1", 192, F4), ("eq", 384, B2), ("lo", 384, F4), ("tx", 16, F4), ("off", 16, U2), ("XE", 256, B2),
        ("nx", 256, I4), ("LR0", 256, F2), ("LR1", 256, F2), ("LR2", 256, F2)] + [("LE%d%d" % ks, 16, F2) for ks in FOREIGN]:
    SCRATCH[_n] = ("sbuf", [128, _w], _d)
SCRATCH["MA"] = ("sbuf", [128, 256, 16], B2)
for _n in ("pA", "pL", "pR", "pS", "pD0", "pD1", "pD2", "pD3"):
    SCRATCH[_n] = ("psum", [128, 512], F4)
SEMAPHORES = (["sv", "sa", "sp", "sq", "dr", "dx", "dw", "dk", "d2", "dy", "dz", "loc"] + ["ar%d" % k for k in range(3)]
              + ["ae%d%d" % ks for ks in FOREIGN])


def rank_program(g, core, T, topo):
    rank = T.rank_of(core)
    if rank is None:
        return
    n_ranks = len(T.cores)
    eng = {"v": g.vector, "a": g.scalar, "p": g.tensor, "q": g, "s": g.sync}
    sem = {"v": "sv", "a": "sa", "p": "sp", "q": "sq"}
    count = {"v": 0, "a": 0, "p": 0, "q": 0}
    know = {e: {} for e in eng}
    lastw, readers, bank = {}, {}, {}

    def need(e, token):
        name, n, clock = token
        if know[e].get(name, 0) >= n:
            return
        eng[e].wait_ge(T.sem[name], n)
        for s_, n_ in list(clock.items()) + [(name, n)]:
            if know[e].get(s_, 0) < n_:
                know[e][s_] = n_

    def before(e, R, W, banks):
        own = sem.get(e)
        deps = [lastw[r] for r in R if r in lastw]
        deps += [lastw[w] for w in W if w in lastw and (e != "p" or lastw[w][0] != own)]
        for w in W:
            deps += [t for t in readers.get(w, []) if t[0] != own]
        for b in banks:
            deps += [t for x, t in bank.get(b, {}).items() if x != e]
        for t in sorted(deps, key=lambda t: -t[1]):
            need(e, t)

    def after(e, token, R, W, banks):
        for w in W:
            lastw[w] = token
            readers[w] = []
        for r in R:
            readers.setdefault(r, []).append(token)
        for b in banks:
            bank.setdefault(b, {})[e] = token

    def op(e, calls, R=(), W=(), B=()):
        before(e, R, W, B)
        for c in (calls if isinstance(calls, list) else [calls]):
            i = c()
        count[e] += 1
        i.then_inc(T.sem[sem[e]], 1)
        after(e, (sem[e], count[e], dict(know[e])), R, W, B)

    def dma(e, out, in_, s, R=(), W=()):
        before(e, R, W, ())
        eng[e].dma_start(out, in_).then_inc(T.sem[s], 16)
        after(e, (s, 16, dict(know[e])), R, W, ())

    V, A, P = g.vector, g.scalar, g.tensor

    def ts(out, in0, s1, op0, R, W, s2=None, op1=None, B=()):
        if op1 is None:
            op("v", lambda: V.tensor_scalar(out, in0, s1, None, op0), R, W, B)
        else:
            op("v", lambda: V.tensor_scalar(out, in0, s1, s2, op0, op1), R, W, B)

    def tt(out, in0, in1, o, R, W, B=()):
        op("v", lambda: V.tensor_tensor(out, in0, in1, o), R, W, B)

    def cp(out, in_, R, W, B=()):
        op("v", lambda: V.tensor_copy(out, in_), R, W, B)

    def act(out, in_, f, R, W, B=(), bias=0.0):
        op("a", lambda: A.activation(out, in_, f, bias=bias), R, W, B)

    def mm(out, lhsT, rhs, start, stop):
        return lambda: P.matmul(out, lhsT, rhs, start, stop)

    def blk(t, q):
        return t[:, 128 * q:128 * q + 128]

    loc = [0]

    def send(k, dst_t, src, s, R):
        dst = T.cores[(rank - 1 - k) % n_ranks]
        rid, pid, _ = topo.addr(dst)
        before("q", R, (), ())
        g.remote_dma(dst_t, src, T.sem[s], T.sem.loc, pid, rid, topo.mask(core, dst))
        loc[0] += len(topo.engines(core, dst))

    def arrived(k, s, key):
        src = T.cores[(rank + 1 + k) % n_ranks]
        lastw[key] = (s, len(topo.engines(src, core)), {})

    def iota(name, pattern, base, cm, cols=None):
        out = T[name][:] if cols is None else T[name][:, cols[0]:cols[1]]
        if name == "colU":
            op("q", lambda: g.iota(out, pattern, base, cm, allow_small_or_imprecise_dtypes=True), W=[name])
        else:
            op("q", lambda: g.iota(out, pattern, base, cm), W=[name])

    dma("s", T.ri[:], T.ring[:], "dr", W=["ri"])
    dma("a", T.wti[:], T.wt[:], "dw", W=["wti"])
    dma("a", T.kpi[:], T.kap[:], "dk", W=["kpi"])
    dma("s", T.X[:, 0:4096], T.x[:], "dx", W=["X"])
    iota("ip", [[0, 1]], 0, 1)
    iota("colU", [[-1, 16]], 0, 1)
    iota("iU", [[16, 8], [0, 16]], 0, 0)
    iota("i16", [[16, 16]], 0, 0)
    iota("iL", [[1, 8], [16, 16]], 0, 0)
    iota("inn", [[1, 128]], 0, 0)
    iota("i32", [[0, 2], [16, 16]], 0, 0)
    iota("i1", [[1, 16]], 0, 0)
    ts(T.ipg[:], T.ip[:], 4, OP.arith_shift_right, ["ip"], ["ipg"])
    ts(T.ipm[:], T.ip[:], 15, OP.bitwise_and, ["ip"], ["ipm"])
    cp(T.pc[:], T.ip[:], ["ip"], ["pc"])
    cp(T.pg[:], T.ipg[:], ["ipg"], ["pg"])
    cp(T.pm[:], T.ipm[:], ["ipm"], ["pm"])
    ts(T.colL[:], T.i16[:], T.pg[:], OP.add, ["i16", "pg"], ["colL"])
    ts(T.is0[:], T.pm[:], 0.0, OP.is_equal, ["pm"], ["is0"])
    ts(T.is1[:], T.pm[:], 1.0, OP.is_equal, ["pm"], ["is1"])
    for q in range(16):
        if q == 9:
            ts(T.r16[:], T.ri[:], -2048.0, OP.add, ["ri"], ["r16"])
        ts(blk(T.U, q), T.iU[:], T.colU[:, q:q + 1], OP.is_equal, ["iU", "colU"], ["U%d" % q])
    for k in range(3):
        send(k, T["LR%d" % k][:], T.r16[:], "ar%d" % k, ["r16"])
        arrived(k, "ar%d" % k, "LR%d" % k)

    dn = [0]
    spread_banks = ["pD0", "pD1", "pD2", "pD3"]

    def spread(src, key, buf, bkey, slot, ages, pairs, copier="a"):
        for j in pairs:
            w = min(2, ages - 2 * j)
            bk = spread_banks[dn[0] % len(spread_banks)]
            dn[0] += 1
            op("p", [mm(T[bk][:, 256 * i:256 * i + 256], blk(T.U, 2 * j + i), src[:], True, True) for i in range(w)],
               [key] + ["U%d" % (2 * j + i) for i in range(w)], [bk], [bk])
            o = buf[:, (slot + 2 * j) * 256:(slot + 2 * j + w) * 256]
            ws = [bkey + "s%d" % (slot + 2 * j + i) for i in range(w)]
            if copier == "v":
                ts(o, T[bk][:, 0:256 * w], 2048.0, OP.add, [bk], ws, B=[bk])
            else:
                act(o, T[bk][:, 0:256 * w], AF.Copy, [bk], ws, [bk], bias=2048.0)

    spread(T.r16, "r16", T.RW, "RW", SO, 16, range(8))
    dma("s", T.RW2[:, S2 * 256:(S2 + 14) * 256], T.RW[:, SO * 256:(SO + 14) * 256], "d2",
        ["RWs%d" % (SO + i) for i in range(14)], ["RW2s%d" % (S2 + i) for i in range(14)])
    for q in range(16):
        ts(blk(T.L, q), T.iL[:], T.colL[:, q:q + 1], OP.is_equal, ["iL", "colL"], ["L"] if q == 15 else ["L_%d" % q])
    ts(T.zz[:, 0:256], T.r16[:], T.is0[:], OP.mult, ["r16", "is0"], ["zz0"])
    ts(T.zz[:, 256:512], T.r16[:], T.is1[:], OP.mult, ["r16", "is1"], ["zz1"])
    op("p", [mm(T.pA[:, 64:96], blk(T.L, q), T.zz[:, q::16], q == 0, q == 15) for q in range(16)], ["zz0", "zz1", "L"], ["pA"], ["pA"])
    cp(T.wf[:], T.wti[:], ["wti"], ["wf"])
    ts(T.wh[:], T.wf[:], 256.0, OP.mult, ["wf"], ["wh"])
    ts(T.wg[:], T.wf[:], 16.0, OP.is_ge, ["wf"], ["wg"], -8192.0, OP.mult)
    ts(T.I16[:], T.inn[:], T.pc[:], OP.is_equal, ["inn", "pc"], ["I16"])
    tt(T.wf[:], T.wh[:], T.wg[:], OP.add, ["wh", "wg"], ["wf"])
    ts(T.LANE[:], T.i32[:], T.pm[:], OP.add, ["i32", "pm"], ["LANE"])
    ts(T.ELI[:], T.pA[:, 64:96], 2048.0, OP.add, ["pA"], ["ELI"], B=["pA"])
    ts(T.WD[:], T.L[:], T.wf[:], OP.mult, ["L", "wf"] + ["L_%d" % q for q in range(15)], ["WD"])
    op("v", lambda: V.memset(T.one[:], 1.0), W=["one"])
    for j in (3, 2, 0, 1):
        op("q", lambda: g.affine_select(T.E[:, 512 * j:512 * j + 512], T.one[:], [[-1, 32], [0, 16]], OP.is_equal, 0.0, -32 * j, 1), ["one"], ["E%d" % j])
    iota("iq", [[0, 8], [1, 16]], 0, 0)
    iota("in3", [[0, 4], [1, 32]], 0, 0, (0, 128))
    iota("in3", [[0, 4], [1, 16]], 16, 0, (128, 192))
    iota("i12", [[2, 4], [0, 2]], 1, 0, (0, 8))
    iota("i12", [[2, 4]], 0, 0, (8, 12))

    def constants(part):
        if part == 0:
            cp(T.kf[:], T.kpi[:], ["kpi"], ["kf"])
            ts(T.kpb[:], T.kpi[:], 1, OP.bitwise_and, ["kpi"], ["kpb"])
            ts(T.kg[:], T.kf[:], 1985.0, OP.is_ge, ["kf"], ["kg"], -4096.0, OP.mult)
            ts(T.kh[:], T.kf[:], 64.0, OP.add, ["kf"], ["kh"])
            ts(T.cc0[:], T.kpb[:], 2048.0, OP.mult, ["kpb"], ["cc0"], -2048.0, OP.add)
            ts(T.odd[:], T.pm[:], 2.0, OP.mult, ["pm"], ["odd"], 65.0, OP.add)
            tt(T.kf[:], T.kh[:], T.kg[:], OP.add, ["kh", "kg"], ["kf"])
            ts(T.AD[:], T.I16[:], T.cc0[:], OP.mult, ["I16", "cc0"], ["AD"])
            ts(T.OD[:], T.I16[:], T.odd[:], OP.mult, ["I16", "odd"], ["OD"])
            ts(T.KD[:], T.I16[:], T.kf[:], OP.mult, ["I16", "kf"], ["KD"])
            cp(T.IB[:], T.I16[:], ["I16"], ["IB"])
            ts(T.NI[:], T.I16[:], -1.0, OP.mult, ["I16"], ["NI"])
            ts(T.PI[:], T.I16[:], 128.0, OP.mult, ["I16"], ["PI"])
        elif part == 1:
            ts(T.MC[:], T.iq[:], 0.03125, OP.mult, ["iq"], ["MC"])
            ts(T.LG[:], T.i16[:], T.pm[:], OP.add, ["i16", "pm"], ["LG"], 16.0, OP.mult)
            ts(T.MI[:], T.I16[:], -128.0, OP.mult, ["I16"], ["MI"])
        else:
            ts(T.ig[:], T.inn[:], 4, OP.arith_shift_right, ["inn"], ["ig"])
            ts(T.pm16[:], T.pm[:], 16.0, OP.add, ["pm"], ["pm16"])
            ts(T.dmE[:], T.pm[:], 4096.0, OP.add, ["pm"], ["dmE"])
            ts(T.dmO[:], T.pm[:], 4112.0, OP.add, ["pm"], ["dmO"])
            ts(T.RS[:], T.iq[:], 0.0, OP.is_equal, ["iq"], ["RS"], 1.0e9, OP.mult)
            ts(T.B16[:], T.ig[:], T.pg[:], OP.is_equal, ["ig", "pg"], ["B16"])
            ts(T.HOLD[:, 0:128], T.in3[:, 0:128], 0.0, OP.is_gt, ["in3"], ["HOLDO"])
            ts(T.HOLD[:, 128:192], T.in3[:, 128:192], 16.0, OP.is_gt, ["in3"], ["HOLDE"])
            ts(T.MK[:], T.in3[:], T.pm16[:], OP.is_ge, ["in3", "pm16"], ["MK"], 8192.0, OP.mult)
            ts(T.HOLD[:, 31:128:32], T.in3[:, 31:128:32], 0.0, OP.mult, ["in3", "dmO"], ["HOLDO"], T.dmO[:], OP.add)
            ts(T.HOLD[:, 143:192:16], T.in3[:, 143:192:16], 0.0, OP.mult, ["in3", "dmE"], ["HOLDE"], T.dmE[:], OP.add)
            ts(T.MK[:], T.MK[:], 2048.0, OP.add, ["MK"], ["MK"])
            cp(T.CL[:], T.i12[:], ["i12"], ["CL"])
            ts(T.OH[:], T.i1[:], T.pm[:], OP.is_equal, ["i1", "pm"], ["OH"])

    def el(s):
        if s >= 0:
            return T.EL[:, 16 * s:16 * s + 16], ["EL%dh%d" % (s, h) for h in range(2)]
        return (T.ELI[:, 0:16] if s == -1 else T.ELI[:, 16:32]), ["ELI"]

    Xw = T.X[:, 0:4096]
    pushed = set()

    def push_foreign(k, s):
        pushed.add((k, s))
        key = "LE%d%d" % (k, s)
        buf, bkey, slot = [(T.RW, "RW", SO + 15 - s), (T.RW, "RW", SO - 17 - s), (T.RW2, "RW2", S2 + 15 - s)][k]
        arrived(k, "ae%d%d" % (k, s), key)
        op("p", [mm(T.pR[:, q:256:16], blk(T.U, q), T[key][:], True, True) for q in range(16)],
           [key] + ["U%d" % q for q in range(16)], ["pR"], ["pR"])
        return lambda: act(buf[:, slot * 256:slot * 256 + 256], T.pR[:, 0:256], AF.Copy, ["pR"], [bkey + "s%d" % slot], ["pR"], bias=2048.0)

    def pkey(name, l0, n):
        return ["%s%d" % (name, c) for c in range(l0 // 16, (l0 + n) // 16)]

    two = [(h, slice(16 * h, 16 * h + 16)) for h in range(2)]
    hw = [slice(0, 128), slice(128, 256)]
    half = [(1, hw[1]), (0, hw[0])]
    eight = [slice(8 * h, 8 * h + 8) for h in range(2)]
    DB = ["pD2", "pA"]
    RB, NB = ["pL", "pR"], ["pD2", "pD3"]
    KB, EB = [("pS", 0), ("pA", 256)], [("pS", 256), ("pA", 128)]

    for t in range(STEPS):
        k = t % 3
        last = t == STEPS - 1
        la, lka = el(t - 1)
        lb, lkb = el(t - 2)
        put = push_foreign(k, t - 1) if t > 0 else None
        cp(T.Ga[:, 0:256], Xw.indirect(la), ["X"] + lka, ["Ga0"])
        if t == 0:
            cp(T.Ga[:, 256:512], Xw.indirect(lb), ["X"] + lkb, ["Ga1"])
            spread(T.LR0, "LR0", T.RW, "RW", SO + 16, 16, range(4))
            constants(0)
        else:
            act(T.Ga[:, 256:512], Xw.indirect(lb), AF.Copy, ["X"] + lkb, ["Ga1"])
            put()
        ms = [mm(T.pA[:, 0:32], T.I16[:], T.LANE[:], True, False)]
        if k == 1:
            ms.append(mm(T.pA[:, 0:32], T.I16[:], T.C4[:], False, False))
        op("p", ms, ["I16", "LANE", "C4"], ["pA"], ["pA"])
        op("p", [mm(T.pA[:, 0:32], blk(T.WD, q), T.Ga[:, q::16], False, q == 15) for q in range(16)], ["WD", "Ga0", "Ga1"], ["pA"], ["pA"])
        for h, w in two:
            cp(T.xi[:, w], T.pA[:, w], ["pA"], ["xi%d" % h], ["pA"])
        for h, w in two:
            ts(T.xj[:, w], T.xi[:, w], 8191, OP.bitwise_and, ["xi%d" % h], ["xj%d" % h])
        for h, w in two:
            cp(T.RL[:, w], T.xj[:, w], ["xj%d" % h], ["RL%d" % h])
        if t == 0:
            spread(T.LR0, "LR0", T.RW, "RW", SO + 16, 16, (4, 5))
            spread(T.LR0, "LR0", T.RW, "RW", SO + 16, 16, (6, 7), "v")
            op("v", lambda: V.memset(T.C4[:], 4096.0), W=["C4"])
        buf, rk, w0 = [(T.RW, "RW", SO - t), (T.RW, "RW", SO - 16 - t), (T.RW2, "RW2", S2 - t)][k]
        slots = [rk + "s%d" % i for i in range(w0, w0 + 32)]
        win = buf[:, w0 * 256:(w0 + 32) * 256]
        for h, w in two:
            ts(T.PQ[:, 256 * h:256 * h + 256], win.indirect(T.RL[:, w]), -2048.0, OP.add, ["RL%d" % h] + slots + [x + "h" for x in slots], ["PQ%d" % h])
            op("p", [mm(T[DB[h]][:, 64:80], blk(T.L, q), T.PQ[:, 256 * h + q:256 * h + 256:16], q == 0, q == 15) for q in range(16)],
               ["PQ%d" % h, "L"], [DB[h]], [DB[h]])
        op("p", [mm(T.pL[:, 0:256], T.KD[:], T.PQ[:, 0:256], True, False), mm(T.pL[:, 0:256], T.OD[:], T.PQ[:, 256:512], False, False),
                 mm(T.pL[:, 0:256], T.AD[:], T.one[:, 0:256], False, True)], ["PQ0", "PQ1", "KD", "OD", "AD", "one"], ["pL"], ["pL"])

        def names(h):
            ts(T.PL[:, two[h][1]], T[DB[h]][:, 64:80], 0.0625, OP.mult, [DB[h]], ["PL%d" % h], 2048.0, OP.add, B=[DB[h]])
        names(0)
        for h, w in half:
            tt(T.pr[:, w], T.PQ[:, w], T.PQ[:, 256 + 128 * h:384 + 128 * h], OP.mult, ["PQ0", "PQ1"], ["pr%d" % h])
        if not last:
            ts(T.flg[:], T.xj[:], 4096.0, OP.is_lt if k == 1 else OP.is_ge, ["xj0", "xj1"], ["flg"])
        names(1)
        for h, w in half:
            ts(T.sh[:, w], T.pr[:, w], 5, OP.arith_shift_right, ["pr%d" % h], ["sh%d" % h])
        for h, w in half:
            tt(T.ci[:, w], T.sh[:, w], T.pL[:, w], OP.add, ["sh%d" % h, "pL"], ["ci%d" % h], ["pL"])
        for h, w in half:
            ts(T.cj[:, w], T.ci[:, w], 4095, OP.bitwise_and, ["ci%d" % h], ["cj%d" % h])
        for h, w in half:
            cp(T.cl[:, w], T.cj[:, w], ["cj%d" % h], ["cl%d" % h])
        if t == 0:
            constants(1)
        for h, w in two:
            act(T.XPQ[:, 256 * h:256 * h + 256], Xw.indirect(T.PL[:, w]), AF.Copy, ["X", "PL%d" % h], ["XPQ%d" % h])
        op("p", [mm(T.pS[:, 0:256], T.IB[:], T.XPQ[:, 0:256], True, False), mm(T.pS[:, 0:256], T.IB[:], T.XPQ[:, 256:512], False, True)],
           ["XPQ0", "XPQ1", "IB"], ["pS"], ["pS"])
        for h, w in half:
            o = T[NB[h]][:, 0:128]
            op("p", [mm(o, T.XPQ[:, w], T.NI[:], True, False), mm(o, T.XPQ[:, 256 + 128 * h:384 + 128 * h], T.NI[:], False, False)],
               ["XPQ0", "XPQ1", "NI"], [NB[h]], [NB[h]])
        for h, w in half:
            act(T.sg[:, w], T.pS[:, w], AF.Sign, ["pS"], ["sg%d" % h], ["pS"], bias=-255.5)
            op("p", mm(T[NB[h]][:, 0:128], T.sg[:, w], T.PI[:], False, True), ["sg%d" % h, "PI"], [NB[h]], [NB[h]])
        for h, w in half:
            act(T.YT[:, w], T[NB[h]][:, 0:128], AF.Copy, [NB[h]], ["YT%d" % h], [NB[h]], bias=128.0)
        if not last:
            op("p", mm(T.pA[:, 160:192], T.one[:, 0:128], T.flg[:], True, True), ["one", "flg"], ["pA"], ["pA"])
            op("a", lambda: A.activation(T.jk[:], T.pA[:, 160:192], AF.Copy, accum_out=T.cntf[:]), ["pA"], ["jk", "cntf"], ["pA"])
        for l0, n in PIECES:
            o, i = T.G[:, 16 * l0:16 * (l0 + n)], Xw.indirect(T.cl[:, l0:l0 + n])
            if (l0, n) in A_PIECES:
                act(o, i, AF.Copy, ["X", "cl%d" % (l0 // 128)], pkey("G", l0, n))
            else:
                cp(o, i, ["X", "cl%d" % (l0 // 128)], pkey("G", l0, n))

        def yexp(s):
            l0, n = PIECES[s]
            bk, h = BANKS[s % len(BANKS)], l0 % 128
            op("p", mm(T[bk][:, 0:16 * n], blk(T.YT, l0 // 128), T.E[:, 16 * h:16 * (h + n)], True, False),
               ["YT%d" % (l0 // 128)] + ["E%d" % j for j in range(h // 32, (h + n + 31) // 32)], [bk], [bk])

        def score(Q):
            kb, o = KB[Q // 2]
            o += 64 * (Q % 2)
            op("p", [mm(T[kb][:, o:o + 64], blk(T.L, q), T.MA[:, 64 * Q + q:64 * Q + 64:16, :], False, Q % 2 == 0 and q == 15)
                     for q in range(16)], ["L"] + pkey("MA", 64 * Q, 64), [kb], [kb])
        for kb, o in KB:
            op("p", mm(T[kb][:, o:o + 128], T.I16[:], T.MC[:], True, False), ["I16", "MC"], [kb], [kb])
        yexp(0)
        yexp(1)
        for s, (l0, n) in enumerate(PIECES):
            bk = BANKS[s % len(BANKS)]
            d = T[bk][:, 0:16 * n]
            op("p", mm(d, T.IB[:], T.G[:, 16 * l0:16 * (l0 + n)], False, True), ["IB"] + pkey("G", l0, n), [bk], [bk])
            act(T.MA[:, l0:l0 + n, :], d, AF.Abs, [bk], pkey("MA", l0, n), [bk])
            for x in YEXP_AT.get(s, ()):
                yexp(x)
            if s in SCORE_AT:
                score(SCORE_AT[s])
        score(0)
        if t == 0:
            constants(2)
            spread_banks[:] = ["pD0", "pD1"]
        if t == 0:
            spread(T.LR1, "LR1", T.RW, "RW", SO - 16, 15, range(4))
        if t == 1:
            spread(T.LR2, "LR2", T.RW2, "RW2", S2 + 16, 14, range(4))

        def count_a(i):
            if i == 0:
                cp(T.cnti[:], T.cntf[:], ["cntf"], ["cnti"])
            elif i == 1:
                ts(T.cnta[:], T.cnti[:], 63, OP.bitwise_and, ["cnti"], ["cnta"])
            elif i == 2:
                tt(T.acc[:], T.cnta[:], T.cc0[:], OP.add, ["cnta", "cc0"], ["acc"])
            else:
                ts(T.AD[:], T.I16[:], T.acc[:], OP.mult, ["I16", "acc"], ["AD"])

        def scan(h):
            kb, o = KB[h]
            op("v", lambda: V.tensor_tensor_scan(T.mn[:, hw[h]], T.RS[:], T[kb][:, o:o + 128], 0.0, OP.max, OP.min), ["RS", kb], ["mn%d" % h], [kb])

        def ki(h):
            ts(T.ki[:, eight[h]], T.mn[:, 128 * h + 15:128 * h + 128:16], 32.0, OP.mult, ["mn%d" % h], ["ki%d" % h])

        def kj(h):
            ts(T.kj[:, eight[h]], T.ki[:, eight[h]], 15, OP.bitwise_and, ["ki%d" % h], ["kj%d" % h])

        def ml(h):
            cp(T.ML[:, eight[h]], T.kj[:, eight[h]], ["kj%d" % h], ["ML%d" % h])

        def c16(h):
            ts(T.c16[:, hw[h]], T.cj[:, hw[h]], -2048.0, OP.add, ["cj%d" % h], ["c16%d" % h])

        def gl(h):
            tt(T.kl[:, eight[h]], T.kj[:, eight[h]], T.LG[:, eight[h]], OP.add, ["kj%d" % h, "LG"], ["kl%d" % h])

        def gl2(h):
            cp(T.GL[:, eight[h]], T.kl[:, eight[h]], ["kl%d" % h], ["GL%d" % h])

        def choose(h):
            w = hw[h]
            tt(T.z[:, w], T.OH[:].indirect(T.ML[:, eight[h]]), T.c16[:, w], OP.mult, ["OH", "ML%d" % h, "c16%d" % h], ["z%d" % h])
            eb, o = EB[h]
            op("p", [mm(T[eb][:, o:o + 8], blk(T.L, q), T.z[:, 128 * h + q:128 * h + 128:16], q == 0, q == 15) for q in range(16)], ["L", "z%d" % h], [eb], [eb])
            rb = T[RB[h]]
            op("p", [mm(rb[:, 0:192], T.I16[:], T.MK[:], True, False), mm(rb[:, 0:128], T.B16[:], T.z[:, w], False, False)]
               + [mm(rb[:, 128 + 16 * b:144 + 16 * b], T.B16[:], T.z[:, 128 * h + 32 * b:128 * h + 32 * b + 16], False, b == 3) for b in range(4)]
               + [mm(rb[:, 256:384], T.B16[:], T.z[:, w], True, True)], ["I16", "MK", "B16", "z%d" % h], [RB[h]], [RB[h]])

        def oldsum(h):
            o, w = T[NB[h]][:, 0:128], hw[h]
            op("p", [mm(o, T.IB[:], T.XPQ[:, w], True, False), mm(o, T.IB[:], T.XPQ[:, 256 + 128 * h:384 + 128 * h], False, False),
                     mm(o, T.MI[:], T.sg[:, w], False, False)], ["IB", "MI", "XPQ0", "XPQ1", "sg%d" % h], [NB[h]], [NB[h]])

        def old(h):
            act(T.XE[:, hw[h]], T.G[:].indirect(T.GL[:, eight[h]]), AF.Copy, pkey("G", 0, 256) + ["GL%d" % h], ["XE%d" % h])
            op("p", mm(T[NB[h]][:, 0:128], T.IB[:], T.XE[:, hw[h]], False, True), ["IB", "XE%d" % h], [NB[h]], [NB[h]])

        def nx(h):
            ts(T.nx[:, hw[h]], T[NB[h]][:, 0:128], 0.5, OP.mult, [NB[h]], ["nx%d" % h], -64.25, OP.add, B=[NB[h]])

        def lists(h):
            eb, o = EB[h]
            ts(T.EL[:, 16 * t + 8 * h:16 * t + 8 * h + 8], T[eb][:, o:o + 8], 2048.0, OP.add, [eb], ["EL%dh%d" % (t, h)], B=[eb])
            ts(T.ewf[:, eight[h]], T[eb][:, o:o + 8], 2048.0, OP.add, [eb], ["ewf%d" % h], B=[eb])
            if not last:
                cp(T.e16[:, 16 * t + 8 * h:16 * t + 8 * h + 8], T[eb][:, o:o + 8], [eb], ["e16%d" % h], [eb])
                if h == 0:
                    for kk in sorted(range(3), key=lambda x: (x - t - 1) % 3):
                        if (kk, t) in FOREIGN:
                            send(kk, T["LE%d%d" % (kk, t)][:], T.e16[:, 16 * t:16 * t + 16], "ae%d%d" % (kk, t), ["e160", "e161"])

        def ex(h):
            act(T["EX%d" % h][:], T.ewf[:, eight[h]].indirect(T.CL[:]), AF.Copy, ["ewf%d" % h, "CL"], ["EX%d" % h])

        def eq(h):
            tt(T.eq[:, 192 * h:192 * h + 192], T["EX%d" % h][:], T[RB[h]][:, 0:192], OP.is_equal, ["EX%d" % h, RB[h]], ["eq%d" % h], [RB[h]])

        def lo(h):
            w = slice(192 * h, 192 * h + 192)
            op("v", lambda: V.tensor_tensor_scan(T.lo[:, w], T.HOLD[:], T.eq[:, w], 0.0, OP.mult, OP.max), ["HOLDO", "HOLDE", "eq%d" % h], ["lo%d" % h])

        def tx(h):
            tt(T.tx[:, 8 * h + 1:8 * h + 8:2], T.lo[:, 192 * h + 31:192 * h + 128:32], T.ewf[:, 8 * h + 1:8 * h + 8:2], OP.max, ["lo%d" % h, "ewf%d" % h], ["txO%d" % h])
            tt(T.tx[:, 8 * h:8 * h + 8:2], T.lo[:, 192 * h + 143:192 * h + 192:16], T.ewf[:, 8 * h:8 * h + 8:2], OP.max, ["lo%d" % h, "ewf%d" % h], ["txE%d" % h])

        def off(h):
            cp(T.off[:, eight[h]], T.tx[:, eight[h]], ["txO%d" % h, "txE%d" % h], ["off%d" % h])

        def scatter(b):
            cp(T.X[:].indirect(T.off[:, 2 * b:2 * b + 2]), T.nx[:, 32 * b:32 * b + 32], ["off%d" % (b // 4), "nx%d" % (b // 4)], ["X"])

        parts = {"count": count_a, "scan": scan, "ki": ki, "kj": kj, "ml": ml, "c16": c16, "gl": gl, "gl2": gl2, "choose": choose,
                 "oldsum": oldsum, "old": old, "nx": nx, "lists": lists, "ex": ex, "eq": eq, "lo": lo, "tx": tx, "off": off, "scatter": scatter}
        for name, h in TAIL:
            if not (last and name == "count"):
                parts[name](h)
        for h in range(2):
            for buf, bkey, slot in [(T.RW, "RW", SO - 1 - t), (T.RW2, "RW2", S2 - 1 - t)][:1 if last else 2]:
                act(buf[:, slot * 256 + 128 * h:slot * 256 + 128 * h + 128], T[RB[h]][:, 256:384], AF.Copy, [RB[h]],
                    [bkey + "s%d%s" % (slot, "" if h else "h")], [RB[h]], bias=2048.0)
        if t == 0:
            spread(T.LR1, "LR1", T.RW, "RW", SO - 16, 15, range(4, 8))
        if t == 1:
            spread(T.LR2, "LR2", T.RW2, "RW2", S2 + 16, 14, range(4, 7))
        if not last:
            for s in range(t):
                if ((t + 1) % 3, s) in FOREIGN and ((t + 1) % 3, s) not in pushed:
                    push_foreign((t + 1) % 3, s)()

    slots = ["RWs%d" % i for i in range(SO - 6, SO + 10)]
    dma("a", T.yr[:], T.RW[0:128:16, (SO - 6) * 256:(SO + 10) * 256], "dz", R=slots + [x + "h" for x in slots])
    dma("s", T.yx[:], T.X[:, 0:4096], "dy", R=["X"])
    for e in ("v", "a", "p", "q"):
        g.wait_ge(T.sem[sem[e]], count[e])
    g.wait_ge(T.sem.loc, loc[0])
    g.wait_ge(T.sem.d2, 16)
    g.wait_ge(T.sem.dz, 16)
    g.wait_ge(T.sem.dy, 16)
